import numpy as np, ml_dtypes
CORES = [5,29,101,125,133,157,229,253]
N = 8
BF = ml_dtypes.bfloat16
def gentries(a):
    return np.ascontiguousarray(a.reshape(8, 16, -1).transpose(0, 2, 1)).reshape(8, -1)
def gtable(e):
    e = np.asarray(e); return np.ascontiguousarray(e.reshape(8, -1, 16).transpose(0, 2, 1)).reshape(128, -1).astype(np.int32)
W, L, S, ST = 2048, 256, 16, 5
def parts(rng):
    x = rng.integers(0, 64, (N, 8, 16, W)); v = rng.integers(0, W, (N, 8, L, S)); c = rng.integers(0, W, (N, 8, L, S))
    n = np.where(rng.random((N, 8, L)) < 0.4, rng.integers(0, 4, (N, 8, L)), rng.integers(4, S + 1, (N, 8, L)))
    return x, v, c, n, rng.integers(220, 460, (N, 8)), rng.integers(0, 256, (N, 8, 16))
def pack(x, v, c, n, th, w):
    return {"xc": np.ascontiguousarray(x.reshape(N, 128, W)).astype(np.float32).astype(BF), "vl": np.stack([gtable(a.reshape(8, -1)) for a in v]), "cl": np.stack([gtable(a.reshape(8, -1)) for a in c]),
            "ln": np.ascontiguousarray(n).astype(np.int32), "th": np.ascontiguousarray(th.reshape(N, 8, 1)).astype(np.int32), "wt": np.ascontiguousarray(w.reshape(N, 128, 1)).astype(np.int32)}
def setup_inputs(rng):
    return pack(*parts(rng))
def setup_inputs_ties(rng):
    x, v, c, n, th, w = parts(rng)
    x = np.repeat(8 * rng.integers(0, 8, (N, 8, 1, W)), 16, axis=2); up = rng.integers(0, 3, (N, 8, W)) * (rng.random((N, 8, W)) < 0.4)
    x = x + up[:, :, None, :] * (np.arange(16)[:, None] == rng.integers(0, 16, (N, 8, 1, W)))
    o = np.argsort(rng.random((N, 8)), axis=1); j = o >> 1; less = np.where(rng.random((N, 8)) < 0.6, rng.integers(0, 2, (N, 8)), rng.integers(0, 32, (N, 8)))
    th = np.maximum(128 * j - less, 0); s = np.arange(S)
    for r in range(N):
        z = 128 * int(rng.integers(4, 7))
        for g, e in ((int(np.argmin(o[r])), 0), (int(np.argmax(o[r])), 1)):
            th[r, g] = z + e
            x[r, g, :, 0] = 0; x[r, g, :, 1] = 56; x[r, g, :, 2] = z >> 4; x[r, g, int(rng.integers(0, 16)), 2] += 1
            v[r, g, 1::2] = np.where(s < 2, 0, 2); c[r, g, 1::2] = np.where(s < 1, 1, 2); n[r, g, 1::2] = rng.integers(4, S + 1, L // 2)
    q = int(rng.integers(0, N)); a = (q - 1) % N; b = (q - 2) % N
    n[a] = np.where(n[a] >= 4, rng.integers(4, 6, (8, L)), n[a])
    n[q] = rng.integers(0, 4, (8, L)); p = rng.permutation(8 * L)[:31]; one = rng.integers(0, W, (31, 1))
    n[q, p // L, p % L] = 4; v[q, p // L, p % L] = one; c[q, p // L, p % L] = one; th[q] = 128 * rng.integers(1, 4, 8) - 16
    x[b, :, :, 16:40:3] = 0; x[b, :, :, 17:40:3] = 56; x[b, :, :, 18:40:3] = 63; x[b, :, :, 64:128] = 8 * rng.integers(0, 2, (8, 1, 64))
    f0 = 16 + 3 * (np.arange(L // 4)[:, None] & 7); far = rng.integers(64, 128, (8, L // 4, S)); e = rng.integers(128, W, (8, L // 4, S))
    v[b, :, ::4] = np.where(s == 0, e, np.where((s == 1) | (s >= S - 3), f0 + 2, np.where(s == 2, f0 + 1, far)))
    c[b, :, ::4] = np.where(s == 0, f0 + 2, np.where((s == 1) | (s == S - 3), f0, rng.integers(128, W, far.shape)))
    n[b, :, ::4] = S
    return pack(x, v, c, n, th, w)
def setup_inputs_alike(rng):
    x, v, c, n, th, w = parts(rng)
    few = np.array([0, W - 1, W // 2, 3, W - 2, 17])
    v[:, ::2] = few[rng.integers(0, 6, (N, 4, L, S))]; v[:, 1::2, :, 0] = few[rng.integers(0, 6, (N, 4, L))]
    w[:, ::2] = 0; th[:, ::2] = rng.integers(0, 260, (N, 4)); th[:, 1::2] = rng.integers(150, 500, (N, 4))
    o = rng.permutation(4); shutting = 2 * int(o[0]); taking = 2 * int(o[1]); growing = 1 + 2 * int(rng.integers(0, 4))
    n[:, growing] = rng.integers(4, S + 1, (N, L)); v[:, growing, :, 0] = few[int(rng.integers(0, 6))]; th[:, growing] = 0
    n[:, shutting] = rng.integers(ST + 3, S + 1, (N, L)); th[:, shutting] = 1008
    rest = np.where(rng.random((N, L)) < 0.8, 0, rng.integers(1, 4, (N, L)))
    n[:, taking] = np.where(np.arange(N)[:, None] % 2 == 0, rng.integers(ST + 3, S + 1, (N, L)), rest); th[:, taking] = 1008
    return pack(x, v, c, n, th, w)
def setup_inputs_corners(rng):
    x, v, c, n, th, w = parts(rng)
    lo = (W - 1) * rng.integers(0, 2, (N, 8, 1)); hi = W - 1 - lo
    x[..., 0] = np.where(lo == 0, 0, 63); x[..., W - 1] = np.where(lo == 0, 63, 0)
    n = rng.choice(np.array([0, 1, 2, 3, 4, 5, S - 1, S]), (N, 8, L)); kind = rng.integers(0, 5, (N, 8, L))
    for g, i in ((0, 0), (7, L - 1)):
        n[0, g, i] = S; kind[0, g, i] = 0; n[1, g, i] = 0
    n[N - 1, 7, L - 2] = S; kind[N - 1, 7, L - 2] = 1
    s = np.arange(S); q = np.maximum(n, 4)[..., None]; kd = kind[..., None]; A = lo[..., None]; H = hi[..., None]
    v0 = np.where((s < 2) | (s == q - 1), H, A); v1 = np.where((s == q - 3) | (s == q - 2), H, A); v2 = np.where(s >= q - 3, H, A)
    one = rng.integers(0, W, (N, 8, L, 1))
    v = np.where(kd == 0, v0, np.where(kd == 1, v1, np.where(kd == 2, v2, np.where(kd == 3, one, v))))
    c = np.where(kd < 3, A, np.where(kd == 3, one, c))
    v = np.where(s < n[..., None], v, (W - 1) * rng.integers(0, 2, v.shape)); c = np.where(s < n[..., None], c, (W - 1) * rng.integers(0, 2, c.shape))
    return pack(x, v, c, n, np.array([0, 5, 500, 900])[np.argsort(rng.random((N, 8)), axis=1) >> 1], w)
def setup_inputs_ends(rng):
    x, v, c, n, th, w = parts(rng)
    e = 63 * rng.integers(0, 2, (N, 8, 1)); e[N - 1, 7] = 0
    x = 63 * rng.integers(0, 2, (N, 8, 16, W)); x[..., 0] = e; x[..., W - 1] = 63 - e
    for j in range(1, 17):
        for col in (j, W - 1 - j):
            x[..., col] = 63 - e; x[:, :, j - 1, col] = np.abs(62 - e[..., 0])
    v = np.where(rng.random(v.shape) < 0.75, (W - 1) * rng.integers(0, 2, v.shape), v); c = np.where(rng.random(c.shape) < 0.75, (W - 1) * rng.integers(0, 2, c.shape), c)
    kind = rng.integers(0, 3, (N, 8, L)); kind[..., 0] = 1; kind[..., L - 1] = 1; kind[..., 1] = 2; kind[..., L - 2] = 2
    k1 = kind == 1; k2 = kind == 2; v[k1 | k2] = W - 1; c[k1] = W - 1
    c = np.where(k2[..., None], (W - 1) * rng.integers(0, 2, c.shape), c)
    near = rng.integers(1, 17, (N, 8, L)); near = np.where(rng.random((N, 8, L)) < 0.5, near, W - 1 - near)
    v[..., 0] = np.where(k1, near, v[..., 0]); c[..., 0] = np.where(k1, 0, c[..., 0]); c[..., S - 3] = np.where(k1 | k2, 0, c[..., S - 3])
    v[..., S - 1] = np.where(k1, (W - 1) * rng.integers(0, 2, (N, 8, L)), v[..., S - 1]); v[N - 1, 7, L - 1, S - 1] = 0
    n = np.where(rng.random((N, 8, L)) < 0.7, S, 0); n[..., 0] = S; n[..., 1] = S; n[..., 2] = 0; n[..., L - 2] = S; n[..., L - 1] = S; n[0, :, L - 1] = 0
    th = 1008 * (np.argsort(rng.random((N, 8)), axis=1) & 1)
    if th[N - 1, 7] > 0: th[N - 1] = 1008 - th[N - 1]
    w = 255 * rng.integers(0, 2, (N, 8, 16)); w[:, 7] = 255; w[:, 0] = 0
    return pack(x, v, c, n, th, w)
def setup_inputs_spread(rng):
    x, v, c, n, th, w = parts(rng)
    x = np.minimum((np.exp2(6.1 * rng.random((N, 8, 1, W))) * rng.random((N, 8, 16, W))).astype(np.int64), 63)
    po = rng.choice(np.array([1.0, 2.0, 4.0]), (N, 8, 1, 1)); v = np.minimum((W * rng.random(v.shape) ** po).astype(np.int64), W - 1); c = np.minimum((W * rng.random(c.shape) ** po[:, ::-1]).astype(np.int64), W - 1)
    n = np.minimum(((S + 1) * rng.random((N, 8, L)) ** rng.choice(np.array([0.5, 1.0, 2.0]), (N, 8, 1))).astype(np.int64), S)
    th = np.minimum(np.exp2(10 * rng.random((N, 8))).astype(np.int64) - 1, 1008); w = np.minimum(np.exp2(8.05 * rng.random((N, 8, 16))).astype(np.int64) - 1, 255)
    return pack(x, v, c, n, th, w)
def check_inputs(d):
    bad = []
    for k, lo, hi in (("xc", 0, 63), ("vl", 0, W - 1), ("cl", 0, W - 1), ("ln", 0, S), ("th", 0, 1008), ("wt", 0, 255)):
        a = np.asarray(d[k]).astype(np.float64)
        if not (np.min(a) >= lo and np.max(a) <= hi): bad.append("range of " + k)
    a = np.asarray(d["xc"]).astype(np.float64)
    if not np.all(np.floor(a) == a): bad.append("xc is not whole")
    return bad
def reference(xc, vl, cl, ln, th, wt):
    X = np.ascontiguousarray(xc.astype(np.float32).astype(np.int32).reshape(N, 8, 16, W).transpose(0, 1, 3, 2))
    V = np.stack([gentries(q) for q in vl]).astype(np.int32).reshape(N, 8, L, S); C = np.stack([gentries(q) for q in cl]).astype(np.int32).reshape(N, 8, L, S)
    n = ln.astype(np.int64).reshape(N, 8, L); lim = th.astype(np.int64).reshape(N, 8, 1, 1); w = wt.astype(np.int64).reshape(N, 8, 1, 16)
    a = np.arange(N)[:, None, None, None]; b = np.arange(8)[None, :, None, None]; s = np.arange(S); shut = np.zeros(N, np.int64)
    for t in range(ST):
        XV = X[a, b, V]; XC = X[a, b, C]; live = n >= 4
        bend = np.add.reduce(np.abs(XV[:, :, :, :-1] + XV[:, :, :, 1:] - 2 * XC[:, :, :, :-1]), axis=-1, dtype=np.int32)
        k = np.argmax(np.where(s[:-1] <= n[..., None] - 3, bend, -1), axis=3)[..., None]
        Vk = np.take_along_axis(V, k, 3); Vn = np.take_along_axis(V, k + 1, 3); Ck = np.take_along_axis(C, k, 3)
        y = np.clip(X[a, b, Vk] + X[a, b, Vn] - X[a, b, Ck], 0, 63)
        dist = np.add.reduce(np.abs(XV - y), axis=-1, dtype=np.int32)
        fit = (s >= k + 2) & (s <= n[..., None] - 1) & (dist <= lim + shut[:, None, None, None]) & live[..., None]
        close = np.any(fit, axis=3); m = np.argmax(fit, axis=3)[..., None]; grow = live & ~close
        size = np.where(close[..., None], m - k - 1, 0)
        ix = np.minimum(k + 1 + s, S - 1); keep = s < size
        PV = np.where(keep, np.take_along_axis(V, ix, 3), 0); PC = np.where(keep, np.take_along_axis(C, ix, 3), 0)
        y = y[:, :, :, 0]; u = np.add.reduce(w * y, axis=-1) & (W - 1)
        h = (((u * u) >> 5) + 37 * Vk[..., 0].astype(np.int64)) & (W - 1)
        src = np.minimum(np.where(s <= k, s, s + size - grow[..., None].astype(np.int64)), S - 1)
        V2 = np.take_along_axis(V, src, 3); C2 = np.take_along_axis(C, src, 3); new = grow[..., None] & (s == k + 1)
        V2 = np.where(new, h[..., None], V2); C2 = np.where(new, Vk, np.where(live[..., None] & (s == k), Vn, C2))
        n2 = np.minimum(n + grow.astype(np.int64), S) - size[..., 0]
        for i in range(L - 1, -1, -1):
            p, q = np.nonzero(grow[:, :, i]); X[p, q, h[p, q, i]] = y[p, q, i]
        d = 1 + t % (N - 1)
        came = np.roll(size, d, axis=0)[..., 0]; yin = np.roll(y, d, axis=0); lin = np.roll(live, d, axis=0)
        take = ~live & (came > n)
        V = np.where(take[..., None], np.roll(PV, d, axis=0), V2); C = np.where(take[..., None], np.roll(PC, d, axis=0), C2); n = np.where(take, came, n2)
        V = np.where(s < n[..., None], V, 0).astype(np.int32); C = np.where(s < n[..., None], C, 0).astype(np.int32)
        has = lin & (n >= 1); old = X.copy()
        for i in range(L - 1, -1, -1):
            p, q = np.nonzero(has[:, :, i]); z = V[p, q, i, 0]; X[p, q, z] = (old[p, q, z] + yin[p, q, i]) >> 1
        shut = np.add.reduce(close.astype(np.int64).reshape(N, -1), axis=1) & 31
    return {"yx": np.ascontiguousarray(X.transpose(0, 1, 3, 2)).reshape(N, 128, W).astype(np.float32).astype(BF), "yv": np.stack([gtable(q.reshape(8, -1)) for q in V]).astype(np.float32),
            "yc": np.stack([gtable(q.reshape(8, -1)) for q in C]).astype(np.float32), "yn": n.astype(np.float32)}

@@ -1,0 +1,785 @@
+import numpy as np
+from concourse.mybir import dt, AluOpType as A, AxisListType, ActivationFunctionType as F
+
+ST = 5
+B2, F4, I4, U2 = "bfloat16", "float32", "int32", "uint16"
+SCRATCH = {}
+
+
+SHAPE = {}
+PLACE = {}
+
+
+def _sb(name, shape, dtype, where="sbuf"):
+    SCRATCH[name] = (where, shape, dtype)
+    SHAPE[name] = shape
+
+
+def _pack(name, width, dtype):
+    box = "box_" + dtype
+    at = SCRATCH[box][1][1] if box in SCRATCH else 0
+    SCRATCH[box] = ("sbuf", [128, at + (width + 15) // 16 * 16], dtype)
+    SHAPE[name] = [128, width]
+    PLACE[name] = (box, at)
+
+
+for _n, _w in (("X", 2304), ("XV", 4112), ("XC", 4096), ("WIN0", 8720), ("WIN1", 8720), ("E", 2048), ("Ev", 2048), ("Ec", 2048),
+               ("wE", 2048), ("Rhi", 2048), ("Rlo", 2048), ("NBm", 2048), ("J32", 2048), ("ID", 128), ("NEGI", 128), ("NEG2", 128), ("BO", 128),
+               ("RV0", 128), ("RV1", 128), ("RS0", 128), ("RS1", 128), ("D01", 128), ("S23", 128), ("REPv", 128), ("ONES", 128),
+               ("RB", 256), ("SEEDP", 256), ("SEEDG", 256), ("SEEDN", 256), ("SEEDS", 256), ("SHS", 256), ("LChi", 256), ("LClo", 256),
+               ("Q0T", 256), ("M1", 256), ("M2", 256), ("PRE", 256), ("SK", 256), ("OH", 256), ("OHG", 256), ("GT", 256), ("SH", 256),
+               ("NS", 256), ("NF", 256), ("MS", 256), ("G1", 256), ("G2", 256), ("G3", 256), ("YT", 256), ("PG1", 256), ("PG2", 256),
+               ("P0", 256), ("CB", 256), ("BS", 256), ("BT", 256), ("N192", 256), ("ZERO", 256), ("LNB", 258), ("HHL", 32), ("CLB", 1)):
+    (_pack if _w <= 258 else lambda n, w, d: _sb(n, [128, w], d))(_n, _w, B2)
+for _n, _w in (("CC", 16), ("KM", 256), ("RF", 256), ("POS0", 256), ("POS1", 256), ("II", 256), ("TPk0", 256), ("TPk1", 256),
+               ("TPn0", 256), ("TPn1", 256), ("IC", 16), ("DD", 16), ("OHT", 256), ("OHPP", 256), ("SRC", 256), ("NN", 16), ("LIVE", 16),
+               ("NR", 16), ("CL", 16), ("GR", 16), ("Ta", 16), ("Tb", 16), ("Td", 16), ("Te", 16), ("QM", 16), ("QN", 16),
+               ("TK", 16), ("HE", 16), ("HF", 16), ("HG", 16), ("HD", 16), ("VG", 16), ("HAS", 16), ("lim", 1), ("thc", 1), ("cls", 1),
+               ("t1", 16), ("FIN", 256), ("VMV", 256), ("VMC", 256), ("AL", 256), ("VKS", 256), ("VNS", 256), ("VKT", 256), ("VNT", 256), ("VF", 16), ("Tc", 16)):
+    _pack(_n, _w, F4)
+_sb("ON", [128, 256], F4)
+for _n, _w in (("VI", 512), ("LNI", 257), ("WTI", 1)):
+    _sb(_n, [128, _w], I4)
+for _n, _w in (("WV", 272), ("WC", 256), ("VJ", 512), ("VL", 512), ("im", 128), ("imh", 128), ("ip", 1), ("ii", 8),
+               ("KI", 16), ("OFI", 16), ("QK", 16), ("OF0", 16), ("UI", 16), ("SQ", 16), ("HI", 16), ("HP", 32), ("ci", 1)):
+    _pack(_n, _w, I4)
+for _n, _w in (("VU", 256), ("CU", 256), ("OFU", 16), ("OFP", 16), ("OFH", 16), ("OFB", 16), ("V0U", 16), ("S0U", 16), ("SRCU", 256),
+               ("HR", 256), ("VR", 256)):
+    _pack(_n, _w, U2)
+_sb("H16", [128, 16], "float16")
+_sb("Rr", [128, 2048], B2)
+_sb("HL", [128, 4, 8, 2, 16], B2)
+_sb("FT", [128, 8, 2, 16], F4)
+_sb("FU", [128, 8, 2, 16], F4)
+_sb("HX", [128, 2, 8, 2, 16], "float16")
+_sb("FO0", [128, 8, 2, 16], F4)
+_sb("FO1", [128, 8, 2, 16], F4)
+_sb("FD", [128, 4, 128], F4)
+_sb("EQ", [128, 16, 256], B2)
+_sb("Z", [128, 16, 256], B2)
+_sb("Z2", [128, 16, 256], B2)
+for _t in range(ST):
+    _sb("YM%d" % _t, [128, 272], B2)
+    _sb("YR%d" % _t, [128, 272], B2)
+    _sb("SM%d" % _t, [128, 48], F4)
+    _sb("SR%d" % _t, [128, 48], F4)
+    _sb("PD%d" % _t, [128, 1024], B2, "dram")
+    _sb("PI%d" % _t, [128, 1024], B2, "dram")
+for _t in range(4):
+    _sb("PZ%d" % _t, [128, 2, 256], F4, "psum")
+for _n in ("PK", "PQ", "PS", "PT"):
+    _sb(_n, [128, 512], F4, "psum")
+SEMAPHORES = ["q_pe", "q_dve", "q_act", "q_g", "loc", "dv", "dc", "dx", "dln", "dwt", "pst", "dout"]
+for _t in range(ST):
+    SEMAPHORES += ["po%d" % _t, "pi%d" % _t, "am%d" % _t, "ay%d" % _t, "as%d" % _t]
+
+_RANGE = {}
+
+
+def _span(name, idx):
+    key = name + repr(idx)
+    if key not in _RANGE:
+        shape = SHAPE[name][1:]
+        a = np.arange(int(np.prod(shape))).reshape(shape)[idx]
+        _RANGE[key] = (int(a.min()), int(a.max()) + 1)
+    return _RANGE[key]
+
+
+def _queues(g, core, T):
+    eng = {"pe": g.tensor, "dve": g.vector, "act": g.scalar, "g": g, "sp": g.sync}
+    cnt = {"pe": 0, "dve": 0, "act": 0, "g": 0}
+    known = {q: {} for q in eng}
+    vc, recs, total = {}, {}, {}
+
+    def V(name, *idx):
+        lo, hi = _span(name, idx) if idx else (0, 1 << 20)
+        if name in PLACE:
+            box, at = PLACE[name]
+            k = idx[0] if idx else slice(0, SHAPE[name][1])
+            return (T[box][:, at + k.start:at + k.stop:k.step or 1], name, lo, hi)
+        return (T[name][(slice(None),) + idx] if idx else T[name][:], name, lo, hi)
+
+    def deps(q, outs, ins, own=None):
+        need = {}
+        for lst, wr in ((ins, 0), (outs, 1)):
+            for (_, name, lo, hi) in lst:
+                psum = SCRATCH.get(name, ("",))[0] == "psum"
+                for r in recs.get(name, ()):
+                    if (q == "pe" and r[4] == "pe") or r[3][0] == own:
+                        continue
+                    if psum and r[4] != q:
+                        hit = True
+                    else:
+                        hit = r[0] < hi and lo < r[1] and (r[2] or wr)
+                    if hit:
+                        s, v = r[3]
+                        if known[q].get(s, 0) < v and need.get(s, 0) < v:
+                            need[s] = v
+        for s in sorted(need):
+            for s2, v2 in need.items():
+                if s2 != s and vc.get((s2, v2), {}).get(s, 0) >= need[s]:
+                    need[s] = 0
+        for s in sorted(need):
+            v = need[s]
+            if v:
+                eng[q].wait_ge(T.sem[s], v)
+                known[q][s] = v
+                for s2, v2 in vc.get((s, v), {}).items():
+                    if known[q].get(s2, 0) < v2:
+                        known[q][s2] = v2
+
+    def note(q, tok, outs, ins):
+        for (_, name, lo, hi) in ins:
+            l = recs.setdefault(name, [])
+            l[:] = [r for r in l if not (not r[2] and r[4] == q and lo <= r[0] and r[1] <= hi)]
+            l.append((lo, hi, 0, tok, q))
+        for (_, name, lo, hi) in outs:
+            l = recs.setdefault(name, [])
+            psum = SCRATCH.get(name, ("",))[0] == "psum"
+            l[:] = [r for r in l if not (lo <= r[0] and r[1] <= hi) or (psum and r[4] != q)]
+            if psum:
+                l[:] = [r for r in l if r[4] == q] + [r for r in l if r[4] != q and known[q].get(r[3][0], 0) < r[3][1]]
+            l.append((lo, hi, 1, tok, q))
+
+    def run(q, call, outs, ins):
+        deps(q, outs, ins)
+        cnt[q] += 1
+        s = "q_" + q
+        call(eng[q]).then_inc(T.sem[s], 1)
+        tok = (s, cnt[q])
+        d = dict(known[q])
+        d[s] = cnt[q]
+        vc[tok] = d
+        note(q, tok, outs, ins)
+
+    def dma(q, sem, n, out, in_):
+        deps(q, [out], [in_], sem)
+        eng[q].dma_start(out[0], in_[0]).then_inc(T.sem[sem], 16)
+        total[sem] = n
+        vc.setdefault((sem, n), dict(known[q]))
+        note("dma", (sem, n), [out], [in_])
+
+    def arrive(name, sem, n):
+        total[sem] = n
+        note("ext", (sem, n), [(None, name, 0, 1 << 20)], [])
+
+    def before(q, ins):
+        deps(q, [], ins)
+
+    def finish():
+        for q in cnt:
+            if cnt[q] and known["g"].get("q_" + q, 0) < cnt[q]:
+                g.wait_ge(T.sem["q_" + q], cnt[q])
+        for s in sorted(total):
+            if known["g"].get(s, 0) < total[s]:
+                g.wait_ge(T.sem[s], total[s])
+
+    return V, run, dma, arrive, before, finish, total
+
+
+def _send(core, T, topo, g, out, in_, arrived, dst):
+    e = topo.engines(core, dst)[:8]
+    rid, pid = topo.addr(dst, core)
+    g.remote_dma(out, in_, T.sem[arrived], T.sem["loc"], pid, rid, sum(1 << k for k in e))
+    return len(e)
+
+
+def _relays(core, dst, topo):
+    if topo.may_write(core, dst):
+        return []
+    c = [k for k in topo.cores_of(core) if k != core and topo.may_write(k, dst)]
+    c.sort(key=lambda k: (topo.die(k) != topo.die(core), k))
+    return [c[0], c[1 % len(c)]]
+
+
+def _relay_program(g, core, T, topo):
+    loc = 0
+    for t in range(ST):
+        for r, src in enumerate(T.cores):
+            dst = T.cores[(r + 1 + t % 7) % len(T.cores)]
+            rl = _relays(src, dst, topo)
+            if core not in rl:
+                continue
+            n = len(topo.engines(src, core)[:8])
+            for k, (name, sem) in enumerate((("PI", "am"), ("YR", "ay"), ("SR", "as"))):
+                if rl[0 if k == 0 else 1] == core:
+                    g.wait_ge(T.sem[sem + str(t)], n)
+                    loc += _send(core, T, topo, g, T[name + str(t)][:], T[name + str(t)][:], sem + str(t), dst)
+    if loc:
+        g.wait_ge(T.sem["loc"], loc)
+
+
+def rank_program(g, core, T, topo):
+    rank = T.rank_of(core)
+    if rank is None:
+        return _relay_program(g, core, T, topo)
+    V, run, dma, arrive, before, finish, total = _queues(g, core, T)
+    n_loc = [0]
+    sl = slice
+    X_ALL, X_WIN = (sl(0, 2304),), (sl(0, 2048),)
+
+    def mm(out, lhsT, rhs, a, z):
+        run("pe", lambda e: e.matmul(out[0], lhsT[0], rhs[0], a, z), [out], [lhsT, rhs])
+
+    def ts(out, in0, s1, op0, s2=None, op1=None):
+        ins = [in0] + [s for s in (s1, s2) if isinstance(s, tuple)]
+        a1 = s1[0] if isinstance(s1, tuple) else s1
+        a2 = s2[0] if isinstance(s2, tuple) else s2
+        if op1 is None:
+            run("dve", lambda e: e.tensor_scalar(out[0], in0[0], a1, None, op0), [out], ins)
+        else:
+            run("dve", lambda e: e.tensor_scalar(out[0], in0[0], a1, a2, op0, op1), [out], ins)
+
+    def tt(out, a, b, op):
+        run("dve", lambda e: e.tensor_tensor(out[0], a[0], b[0], op), [out], [a, b])
+
+    def tc(out, in_):
+        run("dve", lambda e: e.tensor_copy(out[0], in_[0]), [out], [in_])
+
+    def ac(out, in_, f=F.Copy, scale=1.0):
+        ins = [in_] + ([scale] if isinstance(scale, tuple) else [])
+        sc = scale[0] if isinstance(scale, tuple) else scale
+        run("act", lambda e: e.activation(out[0], in_[0], f, scale=sc), [out], ins)
+
+    def scan(out, d0, d1, op0, op1):
+        run("dve", lambda e: e.tensor_tensor_scan(out[0], d0[0], d1[0], 0.0, op0, op1), [out], [d0, d1])
+
+    def fill(out, c):
+        run("dve", lambda e: e.memset(out[0], c), [out], [])
+
+    def iota(out, pattern, base=0, cm=0):
+        run("g", lambda e: e.iota(out[0], pattern, base, cm, allow_small_or_imprecise_dtypes=True), [out], [])
+
+    def gather(q, out, win, off):
+        ap = win[0].indirect(off[0])
+        if q == "act":
+            run("act", lambda e: e.activation(out[0], ap, F.Copy), [out], [win, off])
+        else:
+            run("dve", lambda e: e.tensor_copy(out[0], ap), [out], [win, off])
+
+    def col(k):
+        return V("CC", sl(k, k + 1))
+
+    def small(out, mats, rhs_name, n16):
+        for b in range(16):
+            mm(out, V(mats, sl(b * 128, b * 128 + 128)), V(rhs_name, sl(b, n16, 16)), b == 0, b == 15)
+
+    AND, SHR = A.bitwise_and, A.arith_shift_right
+
+    dma("sp", "dv", 16, V("VI", sl(0, 256)), (T["vl"][:], "vl", 0, 1))
+    dma("sp", "dc", 16, V("VI", sl(256, 512)), (T["cl"][:], "cl", 0, 1))
+    dma("sp", "dx", 16, V("X", sl(0, 2048)), (T["xc"][:], "xc", 0, 1))
+    dma("sp", "dwt", 16, V("WTI"), (T["wt"][:], "wt", 0, 1))
+    fill(V("LNI"), 0)
+    for out_sl, nm in ((sl(0, 256), "ln"), (sl(256, 257), "th")):
+        o = V("LNI", out_sl)
+        dma("sp", "dln", 32, (T["LNI"][0:128:16, out_sl], "LNI", o[2], o[3]), (T[nm][:], nm, 0, 1))
+    iota(V("im"), [[1, 128]])
+    iota(V("ip"), [[0, 1]], 0, 1)
+    iota(V("LClo"), [[0, 16], [16, 16]])
+    iota(V("LChi"), [[256, 16], [0, 16]])
+    iota(V("IC"), [[16, 16]])
+    iota(V("II"), [[16, 16], [0, 16]])
+    iota(V("POS0"), [[16, 16], [-256, 16]], 3840)
+    iota(V("POS1"), [[256, 16], [16, 16]])
+    iota(V("RF"), [[0, 16], [1, 16]])
+    iota(V("WIN0", sl(0, 4368)), [[0, 4368]])
+    iota(V("J32"), [[16, 8], [0, 16], [1, 16]])
+    iota(V("Rlo"), [[0, 2048]])
+
+    i_ = lambda k: V("ii", sl(k, k + 1))
+    ts(i_(0), V("ip"), 15, AND)
+    ts(i_(1), V("ip"), 4, SHR)
+    ts(i_(2), V("ip"), 31, AND)
+    ts(i_(3), V("ip"), 4, SHR, 1, AND)
+    tc(col(0), V("ip"))
+    ts(V("imh"), V("im"), 4, SHR)
+    tc(V("CC", sl(1, 3)), V("ii", sl(0, 2)))
+    tc(col(4), i_(3))
+    ts(col(3), i_(3), -1.0, A.mult, 1.0, A.add)
+    ts(col(5), i_(0), -2.0, A.mult, 15.0, A.add)
+    ts(col(6), i_(2), -2.0, A.mult, 31.0, A.add)
+    ts(V("ID"), V("im"), col(0), A.is_equal)
+    ts(V("CC", sl(5, 7)), V("CC", sl(5, 7)), col(0), A.add)
+    ts(V("BO"), V("imh"), col(2), A.is_equal)
+    ts(col(7), i_(0), 1.5, A.is_le)
+    ts(col(8), i_(0), 3.5, A.is_le)
+    for nm, c, h in (("RV0", 5, 3), ("RV1", 5, 4), ("RS0", 6, 3), ("RS1", 6, 4)):
+        ts(V(nm), V("im"), col(c), A.is_equal, col(h), A.mult)
+    tt(col(8), col(8), col(7), A.subtract)
+    ts(V("NEG2"), V("im"), col(0), A.is_equal, -2.0, A.mult)
+    ac(V("E"), V("X", sl(0, 2048)), F.Copy, 0.0)
+    for k in range(8):
+        ac(V("E", sl(16 * k, 2048, 129)), V("BO", sl(16 * k, 16 * k + 16)))
+    ac(V("Rhi"), V("X", sl(0, 2048)), F.Copy, 0.0)
+    for k in range(2):
+        tc(V("HX", k, sl(0, 8), sl(0, 2), sl(0, 16)), V("VI", sl(256 * k, 256 * k + 256)))
+
+    def payload_in():
+        for k in range(2):
+            h = sl(256 * k, 256 * k + 256)
+            ts(V("VJ", h), V("VI", h), 1792, AND)
+            ts(V("VL", h), V("VI", h), 255, AND)
+            tc(V("HL", 2 * k, sl(0, 8), sl(0, 2), sl(0, 16)), V("VJ", h))
+            tc(V("HL", 2 * k + 1, sl(0, 8), sl(0, 2), sl(0, 16)), V("VL", h))
+        for a in range(4):
+            dma("sp", "pst", 64, (T["PD0"][32 * a:32 * a + 32, :], "PD0", 1024 * a, 1024 * a + 1024), V("HL", a, sl(0, 8), sl(0, 2), sl(0, 16)))
+        for a in range(4):
+            dma("sp", "po0", 64, (T["WIN0"][a:128:16, 16:4112], "WIN0", 16, 4112), (T["PD0"][32 * a:32 * a + 32, :], "PD0", 1024 * a, 1024 * a + 1024))
+
+    for k, dst in enumerate(("VU", "CU")):
+        pz = "PZ%d" % k
+        for kap in range(2):
+            o = V(pz, 0, sl(kap * 128, kap * 128 + 128))
+            for sw in range(2):
+                mm(o, V(("RV%d", "RS%d")[sw] % kap), V("HX", k, sl(0, 8), (kap, 1 - kap)[sw], sl(0, 16)), sw == 0, sw == 1)
+        for kap in range(2):
+            tc(V("FT", sl(0, 8), kap, sl(0, 16)), V(pz, 0, sl(kap * 128, kap * 128 + 128)))
+        tc(V("FIN"), V("FT", sl(0, 8), sl(0, 2), sl(0, 16)))
+        run("dve", lambda e: e.transpose(V("VMV")[0], V("FIN")[0]), [V("VMV")], [V("FIN")])
+        tc(V(dst), V("VMV"))
+        if k == 0:
+            tc(V("WV", sl(16, 272)), V("VMV"))
+    fill(V("WV", sl(0, 16)), 0)
+    fill(V("Z", sl(0, 16), sl(0, 32)), 0.0)
+    fill(V("XV", sl(0, 16)), 0.0)
+
+    def consts_early():
+        tc(col(9), V("WTI"))
+        fill(V("RB"), 1.0)
+        fill(V("RB", sl(0, 256, 16)), 0.0)
+        fill(V("SEEDS"), 1.0)
+        lengths_in()
+        for _ in start_step(0):
+            pass
+        fill(V("Q0T"), 0.0)
+        fill(V("Q0T", sl(0, 256, 16)), 16777216.0)
+        ts(V("LClo"), V("LClo"), col(1), A.add)
+
+    def consts_mid():
+        ts(V("PS", sl(256, 512)), V("RF"), col(1), A.is_gt)
+        tc(V("RF"), V("RB"))
+        ts(V("NEGI"), V("im"), col(0), A.is_equal, -1.0, A.mult)
+        fill(V("SEEDP"), -1.0)
+        fill(V("SEEDP", sl(1, 256, 16)), -65.0)
+        for nm in ("POS0", "POS1", "II", "IC"):
+            ts(V(nm), V(nm), col(1), A.add)
+        ts(V("D01"), V("im"), col(0), A.is_equal, col(7), A.mult)
+        tt(col(10), col(0), col(0), A.subtract)
+        ts(col(10), col(10), 2.0, A.add, col(0), A.add)
+        ts(V("S23"), V("im"), col(10), A.is_equal, col(7), A.mult)
+        ts(V("NBm"), V("J32"), col(0), A.is_equal, -1.0, A.mult)
+        fill(V("Z2", sl(0, 16), sl(224, 256)), 0.0)
+        ts(col(11), col(7), 2048.0, A.mult, col(8), A.add)
+
+    def places(m, grow):
+        tt(V("OHT"), V("II"), V("POS%d" % m), A.subtract)
+        ts(V("TPk%d" % m), V("OHT"), 8192.0, A.add)
+        ts(V("TPn%d" % m), V("OHT"), 8448.0 - grow, A.add)
+
+    def consts_late():
+        ts(V("DD"), V("IC"), 2048.0, A.add)
+        places(0, -256.0)
+        fill(V("SEEDG"), -1.0)
+        fill(V("SEEDG", sl(1, 256, 16)), -65.0)
+        ts(V("t1"), V("im", sl(0, 16)), col(1), A.is_equal)
+        for b in range(16):
+            ts(V("Rr", sl(128 * b, 128 * b + 128)), V("BO"), V("t1", sl(b, b + 1)), A.mult)
+
+    def consts_last():
+        fill(V("SEEDN"), -0.0625)
+        fill(V("SEEDN", sl(1, 256, 16)), 3.9375)
+        places(1, 16.0)
+
+    def lengths_in():
+        tc(V("LNB", sl(0, 256)), V("LNI", sl(0, 256)))
+        ts(V("ci"), V("LNI", sl(256, 257)), 1016, AND)
+        tc(V("LNB", sl(256, 257)), V("ci"))
+        ts(V("ci"), V("LNI", sl(256, 257)), 7, AND)
+        tc(V("LNB", sl(257, 258)), V("ci"))
+        small(V("PS", sl(80, 96)), "E", "LNB", 256)
+        mm(V("PS", sl(96, 97)), V("BO"), V("LNB", sl(256, 257)), True, False)
+        mm(V("PS", sl(96, 97)), V("BO"), V("LNB", sl(257, 258)), False, True)
+        tc(V("NN"), V("PS", sl(80, 96)))
+        tc(V("thc"), V("PS", sl(96, 97)))
+        tc(V("lim"), V("thc"))
+
+    def start_step(t):
+        yield ts(V("LIVE"), V("NN"), 3.5, A.is_ge)
+        yield tt(V("Tb"), V("NN"), V("LIVE"), A.mult)
+        yield ts(V("SEEDS", sl(0, 256, 16)), V("Tb"), -15.0, A.add)
+        yield scan(V("NS"), V("RB"), V("SEEDS"), A.mult, A.add)
+        yield ts(V("M1"), V("NS"), 3.0, A.is_lt, -16777216.0, A.mult)
+        yield ts(V("M2"), V("NS"), 0.5, A.is_le, 8192.0, A.mult)
+        yield tc(V("YM%d" % t, sl(256, 272)), V("LIVE"))
+
+    def push(t, name, out_name, sem, via):
+        dst = T.cores[(rank + 1 + t % 7) % len(T.cores)]
+        rl = _relays(core, dst, topo)
+        to = rl[via] if rl else dst
+        before("g", [V(name)])
+        n_loc[0] += _send(core, T, topo, g, T[out_name][:], T[name][:], sem, to)
+        total["loc"] = n_loc[0]
+
+    def came(t, name, sem):
+        src = T.cores[(rank - 1 - t % 7) % len(T.cores)]
+        rl = _relays(src, core, topo)
+        arrive(name + str(t), sem + str(t), len(topo.engines(rl[0] if rl else src, core)[:8]))
+
+    def dedupe(vict, val1, act, vald, off, cb, meanwhile):
+        tt(V("HE"), val1, act, A.mult)
+        mm(V("PT", sl(256, 512)), V("BO"), V("ZERO"), True, False)
+        for c in range(16):
+            ts(V("EQ", c, sl(0, 256 - 16 * c)), V(vict, sl(16 * c, 256)), V("HE", sl(c, c + 1)), A.is_equal)
+            if c < 15:
+                mm(V("PT", sl(272 + 16 * c, 512)), V("BO"), V("EQ", c, sl(16, 256 - 16 * c)), False, False)
+        d = V("EQ", sl(0, 16), sl(0, 16))
+        tt(V("Te"), vald, act, A.mult)
+        tt(d, d, V("PS", sl(256, 512)), A.mult)
+        if cb != "act":
+            lists_in(0)
+        mm(V("PT", sl(256, 512)), V("BO"), d, False, True)
+        if cb != "act":
+            lists_in(1)
+            if mid[0]:
+                mid[0]()
+                mid[0] = None
+        if cb == "act":
+            ac(V("CB"), V("PT", sl(256, 512)))
+        else:
+            tc(V("CB"), V("PT", sl(256, 512)))
+        small(V("PS", sl(32, 48)), "E", "CB", 256)
+        meanwhile()
+        yield ts(V("Td"), V("PS", sl(32, 48)), 0.5, A.is_lt)
+        yield tt(V("Td"), V("Td"), V("Te"), A.mult)
+        yield tt(V("t1"), V("Td"), V("DD"), A.add)
+        yield tc(V(off), V("t1"))
+
+    def lists_in(j):
+        nxt = now[0]
+        for b in range(16):
+            mm(V("PZ3" if j > 1 else "PZ0", 0, sl(64 * j, 64 * j + 64)), V("Ec", sl(b * 128, b * 128 + 128)), V(nxt, sl(16 + 1024 * j + b, 1040 + 1024 * j, 16)), b == 0, b == 15)
+
+    now, mid = [None], [None]
+
+    def unpack(k):
+        h = sl(128 * k, 128 * k + 128)
+        w = V(("PZ0", "PZ3")[k], 0, h)
+        hv = V("WV", sl(h.start + 16, h.stop + 16))
+        yield ts(hv, w, 2.0 ** -11, A.mult, -0.49976, A.add)
+        yield tc(V("WC", h), w)
+        yield tc(V("VU", h), hv)
+        yield ts(V("WC", h), V("WC", h), 2047, AND)
+        yield tc(V("CU", h), V("WC", h))
+
+    for t in range(ST):
+        cur, nxt = "WIN%d" % (t % 2), "WIN%d" % (1 - t % 2)
+        md = min(t, 1)
+        unit = (256.0, -16.0)[md]
+        S = str(t)
+        ym, sm = "YM" + S, "SM" + S
+
+        def gv(u, n):
+            gather("dve", V("XV", sl(16 + 512 * u, 16 + 512 * u + 512 * n)), V("X", *X_WIN), V("VU", sl(32 * u, 32 * u + 32 * n)))
+
+        def gc(q, u, n):
+            gather(q, V("XC", sl(512 * u, 512 * u + 512 * n)), V("X", *X_WIN), V("CU", sl(32 * u, 32 * u + 32 * n)))
+
+        def bend(u):
+            pz = "PZ%d" % (u % 4)
+            for k in range(2):
+                o = (2 * u + k) * 256
+                for src, mat, a in (("XV", "ID", 16 + o + 32), ("XV", "ID", o + 32), ("XC", "NEG2", o + 32)):
+                    mm(V(pz, k, sl(32, 256)), V(mat), V(src, sl(a, a + 224)), a == 16 + o + 32, src == "XC")
+            ac(V("Z", sl(2 * u, 2 * u + 2), sl(32, 256)), V(pz, sl(0, 2), sl(32, 256)), F.Abs, 4096.0)
+
+        def key(j):
+            o = V("PK", sl(64 * j, 64 * j + 64))
+            for k, m in enumerate(("M1", "Q0T", "LChi", "LClo")):
+                mm(o, V("ID"), V(m, sl(64 * j, 64 * j + 64)), k == 0, False)
+            for b in range(16):
+                mm(o, V("E", sl(b * 128, b * 128 + 128)), V("Z", sl(4 * j, 4 * j + 4), sl(b, 256, 16)), False, b == 15)
+
+        if t:
+            for a in range(4):
+                dma("sp", "po" + S, 64, (T["PD" + S][32 * a:32 * a + 32, :], "PD" + S, 1024 * a, 1024 * a + 1024), (T[cur][a:128:16, 16:4112], cur, 16, 4112))
+            push(t, "PD" + S, "PI" + S, "am" + S, 0)
+        else:
+            iota(V("SHS"), [[0, 256]])
+            iota(V("ZERO"), [[0, 256]])
+            iota(V("ONES"), [[0, 128]], 1)
+            iota(V("N192"), [[0, 256]], -192)
+            iota(V("WIN1", sl(0, 16)), [[0, 16]])
+        gv(0, 1)
+        gv(1, 1)
+        if t == 0:
+            payload_in()
+            push(t, "PD" + S, "PI" + S, "am" + S, 0)
+        gc("act", 0, 1)
+        gc("act", 1, 1)
+        gc("act", 2, 2)
+        gv(2, 2)
+        bend(0)
+        bend(1)
+        bend(2)
+        if t == 0:
+            consts_early()
+        else:
+            st = start_step(t)
+            for _ in unpack(1):
+                next(st)
+            for _ in st:
+                pass
+        gc("act", 4, 2)
+        gv(4, 2)
+        bend(3)
+        gc("act", 6, 1)
+        key(0)
+        gv(6, 2)
+        bend(4)
+        bend(5)
+        key(1)
+        gc("dve" if t else "act", 7, 1)
+        bend(6)
+        bend(7)
+        key(2)
+        if t == 0:
+            ac(V("wE"), V("E"), F.Copy, col(9))
+            consts_mid()
+
+        def dist_x(u):
+            mm(V("PZ%d" % (u % 4), sl(0, 2), sl(0, 256)), V("ID"), V("XV", sl(16 + 512 * u, 528 + 512 * u)), True, False)
+
+        def dist_y(u):
+            pz = "PZ%d" % (u % 4)
+            for k in range(2):
+                c = 2 * u + k
+                mm(V(pz, k, sl(0, 224)), V("YT", sl(128 * (c // 8), 128 * (c // 8) + 128)), V("NBm", sl(256 * (c % 8), 256 * (c % 8) + 224)), False, k == 1)
+            ac(V("Z2", sl(2 * u, 2 * u + 2), sl(0, 224)), V(pz, sl(0, 2), sl(0, 224)), F.Abs)
+
+        def dist_sum(j):
+            o = V("PQ", sl(64 * j, 64 * j + 64))
+            mm(o, V("ID"), V("M2", sl(64 * j, 64 * j + 64)), True, False)
+            mm(o, V("ID"), V("PRE", sl(64 * j, 64 * j + 64)), False, False)
+            for b in range(16):
+                mm(o, V("E", sl(b * 128, b * 128 + 128)), V("Z2", sl(4 * j, 4 * j + 4), sl(b, 256, 16)), False, b == 15)
+
+        dist_x(0)
+        dist_x(1)
+        dist_x(2)
+        key(3)
+        dist_x(3)
+        scan(V("KM"), V("RF"), V("PK", sl(0, 256)), A.mult, A.max)
+        tc(V("KI"), V("KM", sl(15, 256, 16)))
+        ts(V("OFI"), V("KI"), 4095, AND)
+        tc(V("OFU"), V("OFI"))
+        gather("act", V("G3"), V("XC", sl(0, 4096)), V("OFU"))
+        gather("dve", V("G1"), V("XV", sl(16, 4112)), V("OFU"))
+        gather("dve", V("G2"), V("XV", sl(0, 4096)), V("OFU"))
+        yy = (("G1", "ID"), ("G3", "NEGI"), ("G2", "ID"))
+        for h in range(2):
+            for k, (gm, mat) in enumerate(yy):
+                mm(V("PT", sl(256 + 128 * h, 384 + 128 * h)), V(gm, sl(128 * h, 128 * h + 128)), V(mat), k == 0, k == 2)
+        ts(V("QK"), V("OFI"), 4, SHR, 15, AND)
+        ts(V("YT"), V("PT", sl(256, 512)), 0.0, A.max, 63.0, A.min)
+        for u in range(4):
+            dist_y(u)
+        for k, (gm, mat) in enumerate(yy):
+            mm(V("PT", sl(0, 256)), V(mat), V(gm), k == 0, k == 2)
+        ts(V(ym, sl(0, 256)), V("PT", sl(0, 256)), 0.0, A.max, 63.0, A.min)
+        push(t, ym, "YR" + S, "ay" + S, 1)
+        if t == 0:
+            iota(V("WIN0", sl(4368, 8208)), [[0, 3840]])
+        ts(V("SEEDP", sl(0, 256, 16)), V("QK"), 64.0, A.add)
+        scan(V("SK"), V("RB"), V("SEEDP"), A.mult, A.add)
+        ts(V("PRE"), V("SK"), 1.5, A.is_le, 8192.0, A.mult)
+        if t == 0:
+            ts(V("OF0"), V("QK"), -256.0, A.mult, 3840.0, A.add)
+            tt(V("Ta"), V("OF0"), V("IC"), A.add)
+            tc(V("OFP"), V("Ta"))
+        off = ("OFP", "OFU")[md]
+        if t == 0:
+            consts_late()
+        dist_x(4)
+        dist_y(4)
+        dist_x(5)
+        dist_y(5)
+        if t == 0:
+            for k in range(8):
+                ac(V("Rhi", sl(16 * k, 2048, 128)), V("ID", sl(16 * k, 16 * k + 16)))
+                ac(V("Rlo", sl(16 * k + 1, 2048, 128)), V("ID", sl(16 * k, 16 * k + 16)))
+        small(V("PS", sl(16, 32)), "wE", ym, 256)
+        dist_sum(0)
+        p0 = V("PK", sl(0, 256))
+        ts(p0, V("SK"), 0.0, A.is_equal)
+        ts(V("QM"), V("QK"), -16.0, A.add)
+        tt(V("VKS"), p0, V("WV", sl(16, 272)), A.mult)
+        tt(V("VNS"), p0, V("WV", sl(15, 271)), A.mult)
+        scan(V("VKT"), V("RF"), V("VKS"), A.mult, A.add)
+        scan(V("VNT"), V("RF"), V("VNS"), A.mult, A.add)
+        tt(V("OHT"), p0, V("TPk%d" % md), A.mult)
+        tc(V(sm, sl(32, 48)), V("VNT", sl(15, 256, 16)))
+        ts(V(sm, sl(16, 32)), V("QK"), -unit, A.mult, 4096.0 + 16.0 * unit, A.add)
+        tc(V("UI"), V("PS", sl(16, 32)))
+        ts(V("Td"), V("VKT", sl(15, 256, 16)), 37.0, A.mult)
+        ts(V("UI"), V("UI"), 2047, AND)
+        tt(V("SQ"), V("UI"), V("UI"), A.mult)
+        ts(V("SQ"), V("SQ"), 5, SHR)
+        tt(V("HI"), V("SQ"), V("Td"), A.add)
+        ts(V("HI"), V("HI"), 2047, AND)
+        ts(V("HP", sl(0, 16)), V("HI"), 1792, AND)
+        ts(V("HP", sl(16, 32)), V("HI"), 255, AND)
+        tc(V("HHL"), V("HP"))
+        tc(V("H16"), V("HI"))
+        tc(V("HF"), V("HI"))
+        ts(V("HG"), V("HF"), 1.0, A.add)
+        tt(V("HD"), V("HF"), V("DD"), A.subtract)
+        dist_x(6)
+        dist_y(6)
+        dist_sum(1)
+        dist_x(7)
+        dist_y(7)
+        gather("act", V("PG1"), V(cur, sl(16, 4112)), V(off))
+        gather("act", V("PG2"), V(cur, (sl(272, 4368), sl(0, 4096))[md]), V(off))
+        dist_sum(2)
+        dist_sum(3)
+        for b in range(16):
+            mm(V("PT", sl(b, 256, 16)), V("Rr", sl(b * 128, b * 128 + 128)), V("H16"), True, True)
+        ex = V("PK", sl(0, 256))
+        mm(ex, V("D01"), V("PG1"), True, False)
+        mm(ex, V("S23"), V("PG2"), False, True)
+        ph = V("PQ", sl(256, 512))
+        o = V("PK", sl(256, 512))
+        mm(o, V("S23"), V("PG1"), True, False)
+        for b in range(16):
+            for k, mat in enumerate(("Rhi", "Rlo")):
+                mm(V("PK", sl(256 + b, 512, 16)), V(mat, sl(b * 128, b * 128 + 128)), V("HHL", sl(16 * k, 16 * k + 16)), False, b == 15 and k == 1)
+        ac(V(cur, sl(8208, 8720)), V("PK", sl(0, 512)))
+        if t == 0:
+            ac(V("Ec"), V("E"), F.Copy, col(11))
+        ts(V("NF"), V("PQ", sl(0, 256)), V("lim"), A.is_gt)
+        scan(V("MS"), V("NF"), V("NF"), A.mult, A.add)
+        M = V("MS", sl(15, 256, 16))
+        ts(V("CL"), M, 15.5, A.is_le)
+        tt(V("Ta"), M, V("QM"), A.add)
+        SZ = V(sm, sl(0, 16))
+        tt(SZ, V("Ta"), V("CL"), A.mult)
+        push(t, sm, "SR" + S, "as" + S, 1)
+        tt(V("GR"), V("LIVE"), V("CL"), A.subtract)
+        ts(V("HR"), V("PT", sl(0, 256)), 1.0, A.add)
+
+        def own():
+            ts(V("Tb"), V("GR"), -256.0, A.mult, 320.0, A.add)
+            tt(V("SEEDG", sl(0, 256, 16)), V("Tb"), V("QK"), A.add)
+            tt(V("Ta"), SZ, V("GR"), A.subtract)
+            scan(V("OHG"), V("RB"), V("SEEDG"), A.mult, A.add)
+            ts(V("Tb"), V("Ta"), unit, A.mult)
+            ts(V("NR"), V("LIVE"), 99.0, A.mult)
+            ts(ph, V("OHG"), 1.0, A.is_equal)
+            tt(V("OHPP"), V("OHT"), V("POS%d" % md), A.add)
+            tt(V("NR"), V("NR"), V("NN"), A.add)
+            ts(V("QN"), V("QK"), 0.0625, A.mult, -4.0, A.add)
+
+            run("dve", lambda e: e.tensor_reduce(V("cls")[0], V("CL")[0], AxisListType.X, A.add), [V("cls")], [V("CL")])
+            tc(V("CLB"), V("cls"))
+            mm(V("PS", sl(64, 65)), V("ONES"), V("CLB"), True, True)
+
+        dd = dedupe("HR", V("HG"), V("GR"), V("HD"), "OFH", "act", own)
+        next(dd)
+        tt(ph, ph, V("TPn%d" % md), A.mult)
+        tt(V("NN"), V("NN"), V("GR"), A.add)
+        next(dd)
+        tt(V("OHPP"), ph, V("OHPP"), A.add)
+        tc(V("ci"), V("PS", sl(64, 65)))
+        ts(V("NN"), V("NN"), 16.0, A.min)
+        xw = V("X", *X_ALL)
+        put = lambda: run("dve", lambda e: e.tensor_copy(xw[0].indirect(V("OFH")[0]), T[ym][:, 0:256]), [xw], [V("OFH"), V(ym, sl(0, 256))])
+        ts(V("ci"), V("ci"), 31, AND)
+        tt(V("NN"), V("NN"), SZ, A.subtract)
+        if t == 0:
+            consts_last()
+        came(t, "PI", "am")
+        came(t, "YR", "ay")
+        came(t, "SR", "as")
+        if t == 0:
+            iota(V("WIN1", sl(4112, 8208)), [[0, 4096]])
+        for a in range(4):
+            dma("sp", "pi" + S, 64, (T[cur][a:128:16, 4112:8208], cur, 4112, 8208), (T["PI" + S][32 * a:32 * a + 32, :], "PI" + S, 1024 * a, 1024 * a + 1024))
+        sr = V("SR" + S, sl(0, 16))
+        tt(V("TK"), sr, V("NR"), A.is_gt)
+        v0 = V("WV", sl(31, 272, 16))
+        tt(V("Tc"), V("SR" + S, sl(32, 48)), v0, A.subtract)
+        next(dd)
+        tt(V("SEEDN", sl(0, 256, 16)), V("QN"), V("TK"), A.add)
+        tt(V("Tc"), V("Tc"), V("TK"), A.mult)
+        tt(V("Ta"), V("SR" + S, sl(16, 32)), V("TK"), A.mult)
+        scan(V("SK"), V("RB"), V("SEEDN"), A.mult, A.add)
+        tt(V("VF"), v0, V("Tc"), A.add)
+        tt(V("SHS", sl(0, 256, 16)), V("Ta"), V("Tb"), A.add)
+        ts(V("GT"), V("SK"), 0.03, A.is_gt)
+        tc(V("H16"), V("VF"))
+        scan(ph, V("GT"), V("SHS"), A.mult, A.add)
+        tt(V("Ta"), sr, V("NN"), A.subtract)
+        next(dd)
+        tt(V("SRC"), V("OHPP"), ph, A.add)
+        tt(V("Ta"), V("Ta"), V("TK"), A.mult)
+        ts(V("VG"), V("VF"), 1.0, A.add)
+        ts(V("SRCU"), V("SRC"), 8703.0, A.min)
+        tt(V("NN"), V("NN"), V("Ta"), A.add)
+        tt(V("HD"), V("VF"), V("DD"), A.subtract)
+        tc(V("V0U"), V("VF"))
+        ts(V("HAS"), V("NN"), 0.5, A.is_ge)
+        win = V(cur, sl(16, 8720))
+        for b in range(16):
+            mm(V("PT", sl(b, 256, 16)), V("Rr", sl(b * 128, b * 128 + 128)), V("H16"), True, True)
+        for j in range(4):
+            gather("act", V(nxt, sl(16 + 1024 * j, 1040 + 1024 * j)), win, V("SRCU", sl(64 * j, 64 * j + 64)))
+        tt(V("HAS"), V("HAS"), V("YR" + S, sl(256, 272)), A.mult)
+        ts(V("VR"), V("PT", sl(0, 256)), 1.0, A.add)
+        tt(V("lim"), V("ci"), V("thc"), A.add)
+        mid[0] = put
+
+        now[0] = nxt
+
+        def blend_in():
+            run("dve", lambda e: e.tensor_tensor(V("BS")[0], T["X"][:, 0:2048].indirect(V("V0U")[0]), T["YR" + S][:, 0:256], A.add),
+                [V("BS")], [V("X", *X_WIN), V("V0U"), V("YR" + S, sl(0, 256))])
+            ts(V("BT"), V("BS"), 0.5, A.mult, 191.75, A.add)
+
+        dd = dedupe("VR", V("VG"), V("HAS"), V("HD"), "OFB", "dve", blend_in)
+        next(dd)
+        for _ in unpack(0):
+            next(dd, None)
+        run("dve", lambda e: e.tensor_tensor(xw[0].indirect(V("OFB")[0]), V("BT")[0], V("N192")[0], A.add),
+            [xw], [V("OFB"), V("BT"), V("N192")])
+        for j in range(2, 4):
+            lists_in(j)
+    dma("sp", "dout", 64, (T["yx"][:], "yx", 0, 1), V("X", sl(0, 2048)))
+    for k, nm in enumerate(("RV0", "RV1", "RS0", "RS1")):
+        ac(V("FD", k, sl(0, 128)), V(nm))
+    ts(V("SEEDS", sl(0, 256, 16)), V("NN"), -15.0, A.add)
+    scan(V("NS"), V("RB"), V("SEEDS"), A.mult, A.add)
+    ts(V("AL"), V("NS"), 0.5, A.is_gt)
+    tc(V("HHL", sl(0, 16)), V("NN"))
+    for _ in unpack(1):
+        pass
+    tt(V("VMV"), V("WV", sl(16, 272)), V("AL"), A.mult)
+    tt(V("VMC"), V("WC"), V("AL"), A.mult)
+    for b in range(16):
+        mm(V("PT", sl(b, 256, 16)), V("Rhi", sl(b * 128, b * 128 + 128)), V("HHL", sl(0, 16)), True, True)
+    ac(V("ON"), V("PT", sl(0, 256)))
+    dma("sp", "dout", 64, (T["yn"][:], "yn", 0, 1), (T["ON"][0:128:16, :], "ON", 0, 256))
+    fin, ft = ("FIN", "OHT"), ("FT", "FU")
+    for k, vm in enumerate(("VMV", "VMC")):
+        run("dve", lambda e: e.transpose(V(fin[k])[0], V(vm)[0]), [V(fin[k])], [V(vm)])
+    for k in range(2):
+        tc(V(ft[k], sl(0, 8), sl(0, 2), sl(0, 16)), V(fin[k]))
+        for eta in range(2):
+            o = V("PZ%d" % k, 0, sl(eta * 128, eta * 128 + 128))
+            mm(o, V("FD", eta, sl(0, 128)), V(ft[k], sl(0, 8), eta, sl(0, 16)), True, False)
+            mm(o, V("FD", 2 + eta, sl(0, 128)), V(ft[k], sl(0, 8), 1 - eta, sl(0, 16)), False, True)
+    for k, y in enumerate(("yv", "yc")):
+        for eta in range(2):
+            tc(V("FO%d" % k, sl(0, 8), eta, sl(0, 16)), V("PZ%d" % k, 0, sl(eta * 128, eta * 128 + 128)))
+        dma("sp", "dout", 64, (T[y][:], y, 0, 1), V("FO%d" % k, sl(0, 8), sl(0, 2), sl(0, 16)))
+    finish()

@@ -2,10 +2,8 @@ import numpy as np
 from concourse.mybir import dt, AluOpType as A, AxisListType, ActivationFunctionType as F
 
 ST = 5
-B2, F4, I4, U2 = "bfloat16", "float32", "int32", "uint16"
+B2, F4, I4, U2, H2 = "bfloat16", "float32", "int32", "uint16", "float16"
 SCRATCH = {}
-
-
 SHAPE = {}
 PLACE = {}
 
@@ -23,55 +21,70 @@ def _pack(name, width, dtype):
     PLACE[name] = (box, at)
 
 
-for _n, _w in (("X", 2304), ("XV", 4112), ("XC", 4096), ("WIN0", 8720), ("WIN1", 8720), ("E", 2048), ("Ev", 2048), ("Ec", 2048),
-               ("wE", 2048), ("Rhi", 2048), ("Rlo", 2048), ("NBm", 2048), ("J32", 2048), ("ID", 128), ("NEGI", 128), ("NEG2", 128), ("BO", 128),
-               ("RV0", 128), ("RV1", 128), ("RS0", 128), ("RS1", 128), ("D01", 128), ("S23", 128), ("REPv", 128), ("ONES", 128),
-               ("RB", 256), ("SEEDP", 256), ("SEEDG", 256), ("SEEDN", 256), ("SEEDS", 256), ("SHS", 256), ("LChi", 256), ("LClo", 256),
-               ("Q0T", 256), ("M1", 256), ("M2", 256), ("PRE", 256), ("SK", 256), ("OH", 256), ("OHG", 256), ("GT", 256), ("SH", 256),
-               ("NS", 256), ("NF", 256), ("MS", 256), ("G1", 256), ("G2", 256), ("G3", 256), ("YT", 256), ("PG1", 256), ("PG2", 256),
-               ("P0", 256), ("CB", 256), ("BS", 256), ("BT", 256), ("N192", 256), ("ZERO", 256), ("LNB", 258), ("HHL", 32), ("CLB", 1)):
+for _n, _w in (("X", 2304), ("E", 2048), ("Ec", 2048), ("E8", 2048),
+               ("wE", 2048), ("Rhi", 2048), ("Rlo", 2048), ("Rr", 2048), ("ID", 128), ("NEGI", 128), ("ID2", 128), ("NEGH", 128), ("IDK", 128), ("BO", 128),
+               ("RV0", 128), ("RV1", 128), ("RS0", 128), ("RS1", 128), ("D01", 128), ("S23", 128), ("ONES", 128), ("G8", 128), ("STA", 128),
+               ("RB", 256), ("SEEDP", 256), ("SEEDG", 256), ("SEEDS", 256), ("SHS", 256), ("LC", 256),
+               ("M2", 256), ("PRE", 256), ("OHG", 256), ("DM", 256), ("EQD", 256),
+               ("NF", 256), ("MS", 256), ("G1", 256), ("G2", 256), ("G3", 256), ("PG1", 256), ("PG2", 256),
+               ("CB", 256), ("BS", 256), ("BT", 256), ("N192", 256), ("LNB", 258), ("HHL", 32), ("CLB", 1), ("NG", 16), ("NH", 16)):
     (_pack if _w <= 258 else lambda n, w, d: _sb(n, [128, w], d))(_n, _w, B2)
+for _n in ("M1", "NS", "SK", "GT", "Q0N", "SHF"):
+    _pack(_n, 256, B2)
 for _n, _w in (("CC", 16), ("KM", 256), ("RF", 256), ("POS0", 256), ("POS1", 256), ("II", 256), ("TPk0", 256), ("TPk1", 256),
-               ("TPn0", 256), ("TPn1", 256), ("IC", 16), ("DD", 16), ("OHT", 256), ("OHPP", 256), ("SRC", 256), ("NN", 16), ("LIVE", 16),
-               ("NR", 16), ("CL", 16), ("GR", 16), ("Ta", 16), ("Tb", 16), ("Td", 16), ("Te", 16), ("QM", 16), ("QN", 16),
-               ("TK", 16), ("HE", 16), ("HF", 16), ("HG", 16), ("HD", 16), ("VG", 16), ("HAS", 16), ("lim", 1), ("thc", 1), ("cls", 1),
-               ("t1", 16), ("FIN", 256), ("VMV", 256), ("VMC", 256), ("AL", 256), ("VKS", 256), ("VNS", 256), ("VKT", 256), ("VNT", 256), ("VF", 16), ("Tc", 16)):
+               ("TPn0", 256), ("TPn1", 256), ("IC", 16), ("DD", 16), ("OHT", 256), ("OHPP", 256), ("REST", 16), ("R84", 16), ("RS", 16), ("NT", 16), ("NN", 16), ("LIVE", 16),
+               ("NR", 16), ("CL", 16), ("GR", 16), ("Ta", 16), ("Tb", 16), ("Td", 16), ("Te", 16), ("QM", 16),
+               ("TK", 16), ("HE", 16), ("HG", 16), ("HAS", 16), ("A0", 16), ("DAB", 16), ("lim", 1), ("thc", 1), ("cls", 1),
+               ("t1", 16), ("FIN", 256), ("VMV", 256), ("VMC", 256), ("AL", 256), ("VKS", 256), ("VNS", 256), ("VKT", 256), ("VNT", 256),
+               ("Tc", 16), ("HEM", 256), ("SDM", 256), ("DD1", 16), ("OFS", 256)):
     _pack(_n, _w, F4)
 _sb("ON", [128, 256], F4)
 for _n, _w in (("VI", 512), ("LNI", 257), ("WTI", 1)):
     _sb(_n, [128, _w], I4)
-for _n, _w in (("WV", 272), ("WC", 256), ("VJ", 512), ("VL", 512), ("im", 128), ("imh", 128), ("ip", 1), ("ii", 8),
+for _n, _w in (("WV", 272), ("WC", 256), ("VJ", 512), ("VL", 512), ("im", 128), ("imh", 128), ("ip", 1), ("ii", 8), ("i8", 8),
                ("KI", 16), ("OFI", 16), ("QK", 16), ("OF0", 16), ("UI", 16), ("SQ", 16), ("HI", 16), ("HP", 32), ("ci", 1)):
     _pack(_n, _w, I4)
-for _n, _w in (("VU", 256), ("CU", 256), ("OFU", 16), ("OFP", 16), ("OFH", 16), ("OFB", 16), ("V0U", 16), ("S0U", 16), ("SRCU", 256),
-               ("HR", 256), ("VR", 256)):
+for _n, _w in (("VU", 256), ("CU", 256), ("OFU", 16), ("OFN", 16), ("OFP", 16), ("OFH", 16), ("OFB", 16), ("V0U", 16), ("SRCU", 208), ("SRCL", 48),
+               ("HR", 256), ("VR", 256), ("OFG", 8)):
     _pack(_n, _w, U2)
-_sb("H16", [128, 16], "float16")
-_sb("Rr", [128, 2048], B2)
+_sb("H16", [128, 16], H2)
+_sb("V16", [128, 16], H2)
 _sb("HL", [128, 4, 8, 2, 16], B2)
 _sb("FT", [128, 8, 2, 16], F4)
 _sb("FU", [128, 8, 2, 16], F4)
-_sb("HX", [128, 2, 8, 2, 16], "float16")
+_sb("HX", [128, 2, 8, 2, 16], H2)
 _sb("FO0", [128, 8, 2, 16], F4)
 _sb("FO1", [128, 8, 2, 16], F4)
 _sb("FD", [128, 4, 128], F4)
 _sb("EQ", [128, 16, 256], B2)
-_sb("Z", [128, 16, 256], B2)
-_sb("Z2", [128, 16, 256], B2)
+_sb("EV", [128, 16, 256], B2)
+_sb("WIN", [128, 8704], B2)
+_sb("XV", [128, 4096], B2)
+_sb("XC", [128, 4096], B2)
+_sb("SRC", [128, 16, 16], F4)
+_sb("SRT", [128, 16, 3], F4)
+_sb("NLa", [128, 3328], B2)
+_sb("NLb", [128, 768], B2)
+for _n in ("Z", "Z2"):
+    _sb(_n, [128, 16, 16, 16], B2)
 for _t in range(ST):
     _sb("YM%d" % _t, [128, 272], B2)
     _sb("YR%d" % _t, [128, 272], B2)
-    _sb("SM%d" % _t, [128, 48], F4)
-    _sb("SR%d" % _t, [128, 48], F4)
-    _sb("PD%d" % _t, [128, 1024], B2, "dram")
-    _sb("PI%d" % _t, [128, 1024], B2, "dram")
+    _sb("SM%d" % _t, [128, 16], F4)
+    _sb("SR%d" % _t, [128, 16], F4)
+    _sb("KM%d" % _t, [128, 32], F4)
+    _sb("KR%d" % _t, [128, 32], F4)
+    _sb("PD%d" % _t, [128, 4, 256], B2, "dram")
+    _sb("PI%d" % _t, [128, 4, 256], B2, "dram")
 for _t in range(4):
-    _sb("PZ%d" % _t, [128, 2, 256], F4, "psum")
-for _n in ("PK", "PQ", "PS", "PT"):
+    _sb("PZ%d" % _t, [128, 16, 2, 16], F4, "psum")
+_sb("PQ", [128, 16, 32], F4, "psum")
+for _n in ("PK", "PS", "PT"):
     _sb(_n, [128, 512], F4, "psum")
-SEMAPHORES = ["q_pe", "q_dve", "q_act", "q_g", "loc", "dv", "dc", "dx", "dln", "dwt", "pst", "dout"]
+SEMAPHORES = ["q_pe", "q_dve", "q_act", "q_g", "loc", "dv", "dc", "dx", "dln", "dwt", "pst", "dout", "de8"]
 for _t in range(ST):
-    SEMAPHORES += ["po%d" % _t, "pi%d" % _t, "am%d" % _t, "ay%d" % _t, "as%d" % _t]
+    SEMAPHORES += ["po%d" % _t, "pw%d" % _t, "pi%d" % _t, "am%d" % _t, "ay%d" % _t, "as%d" % _t, "ak%d" % _t]
+SENT = (("PI", "am", 0), ("YR", "ay", 1), ("KR", "ak", 1), ("SR", "as", 1))
 
 _RANGE = {}
 
@@ -81,8 +94,12 @@ def _span(name, idx):
     if key not in _RANGE:
         shape = SHAPE[name][1:]
         a = np.arange(int(np.prod(shape))).reshape(shape)[idx]
-        _RANGE[key] = (int(a.min()), int(a.max()) + 1)
+        _RANGE[key] = (sum(1 << int(k) for k in a.ravel()), None)
     return _RANGE[key]
+
+
+def _bits(lo, hi):
+    return lo if hi is None else (1 << min(hi, 16384)) - (1 << lo)
 
 
 def _queues(g, core, T):
@@ -104,13 +121,14 @@ def _queues(g, core, T):
         for lst, wr in ((ins, 0), (outs, 1)):
             for (_, name, lo, hi) in lst:
                 psum = SCRATCH.get(name, ("",))[0] == "psum"
+                m = _bits(lo, hi)
                 for r in recs.get(name, ()):
                     if (q == "pe" and r[4] == "pe") or r[3][0] == own:
                         continue
                     if psum and r[4] != q:
                         hit = True
                     else:
-                        hit = r[0] < hi and lo < r[1] and (r[2] or wr)
+                        hit = r[0] & m and (r[2] or wr)
                     if hit:
                         s, v = r[3]
                         if known[q].get(s, 0) < v and need.get(s, 0) < v:
@@ -131,15 +149,17 @@ def _queues(g, core, T):
     def note(q, tok, outs, ins):
         for (_, name, lo, hi) in ins:
             l = recs.setdefault(name, [])
-            l[:] = [r for r in l if not (not r[2] and r[4] == q and lo <= r[0] and r[1] <= hi)]
-            l.append((lo, hi, 0, tok, q))
+            m = _bits(lo, hi)
+            l[:] = [r for r in l if not (not r[2] and r[4] == q and not r[0] & ~m)]
+            l.append((m, 0, 0, tok, q))
         for (_, name, lo, hi) in outs:
             l = recs.setdefault(name, [])
             psum = SCRATCH.get(name, ("",))[0] == "psum"
-            l[:] = [r for r in l if not (lo <= r[0] and r[1] <= hi) or (psum and r[4] != q)]
+            m = _bits(lo, hi)
+            l[:] = [r for r in l if r[0] & ~m or (psum and r[4] != q)]
             if psum:
                 l[:] = [r for r in l if r[4] == q] + [r for r in l if r[4] != q and known[q].get(r[3][0], 0) < r[3][1]]
-            l.append((lo, hi, 1, tok, q))
+            l.append((m, 0, 1, tok, q))
 
     def run(q, call, outs, ins):
         deps(q, outs, ins)
@@ -201,8 +221,8 @@ def _relay_program(g, core, T, topo):
             if core not in rl:
                 continue
             n = len(topo.engines(src, core)[:8])
-            for k, (name, sem) in enumerate((("PI", "am"), ("YR", "ay"), ("SR", "as"))):
-                if rl[0 if k == 0 else 1] == core:
+            for name, sem, via in SENT:
+                if rl[via] == core:
                     g.wait_ge(T.sem[sem + str(t)], n)
                     loc += _send(core, T, topo, g, T[name + str(t)][:], T[name + str(t)][:], sem + str(t), dst)
     if loc:
@@ -216,13 +236,14 @@ def rank_program(g, core, T, topo):
     V, run, dma, arrive, before, finish, total = _queues(g, core, T)
     n_loc = [0]
     sl = slice
+    ALL = sl(0, 16)
     X_ALL, X_WIN = (sl(0, 2304),), (sl(0, 2048),)
 
     def mm(out, lhsT, rhs, a, z):
         run("pe", lambda e: e.matmul(out[0], lhsT[0], rhs[0], a, z), [out], [lhsT, rhs])
 
-    def ts(out, in0, s1, op0, s2=None, op1=None):
-        ins = [in0] + [s for s in (s1, s2) if isinstance(s, tuple)]
+    def ts(out, in0, s1, op0, s2=None, op1=None, more=()):
+        ins = [in0] + [s for s in (s1, s2) if isinstance(s, tuple)] + list(more)
         a1 = s1[0] if isinstance(s1, tuple) else s1
         a2 = s2[0] if isinstance(s2, tuple) else s2
         if op1 is None:
@@ -230,14 +251,14 @@ def rank_program(g, core, T, topo):
         else:
             run("dve", lambda e: e.tensor_scalar(out[0], in0[0], a1, a2, op0, op1), [out], ins)
 
-    def tt(out, a, b, op):
-        run("dve", lambda e: e.tensor_tensor(out[0], a[0], b[0], op), [out], [a, b])
+    def tt(out, a, b, op, more=()):
+        run("dve", lambda e: e.tensor_tensor(out[0], a[0], b[0], op), [out], [a, b] + list(more))
 
     def tc(out, in_):
         run("dve", lambda e: e.tensor_copy(out[0], in_[0]), [out], [in_])
 
-    def ac(out, in_, f=F.Copy, scale=1.0):
-        ins = [in_] + ([scale] if isinstance(scale, tuple) else [])
+    def ac(out, in_, f=F.Copy, scale=1.0, more=()):
+        ins = [in_] + ([scale] if isinstance(scale, tuple) else []) + list(more)
         sc = scale[0] if isinstance(scale, tuple) else scale
         run("act", lambda e: e.activation(out[0], in_[0], f, scale=sc), [out], ins)
 
@@ -250,19 +271,33 @@ def rank_program(g, core, T, topo):
     def iota(out, pattern, base=0, cm=0):
         run("g", lambda e: e.iota(out[0], pattern, base, cm, allow_small_or_imprecise_dtypes=True), [out], [])
 
-    def gather(q, out, win, off):
-        ap = win[0].indirect(off[0])
+    def at(win, off):
+        return (win[0].indirect(off[0]),) + win[1:]
+
+    def gather(q, out, win, off, scale=1.0):
         if q == "act":
-            run("act", lambda e: e.activation(out[0], ap, F.Copy), [out], [win, off])
+            ac(out, at(win, off), F.Copy, scale, [off])
+        elif scale != 1.0:
+            ts(out, at(win, off), scale, A.mult, more=[off])
         else:
-            run("dve", lambda e: e.tensor_copy(out[0], ap), [out], [win, off])
+            run("dve", lambda e: e.tensor_copy(out[0], at(win, off)[0]), [out], [win, off])
 
     def col(k):
         return V("CC", sl(k, k + 1))
 
+    def top8(name, lo, hi):
+        if name in PLACE:
+            box, a = PLACE[name]
+            return (T[box][0:8, a + lo:a + hi], name, lo, hi)
+        return (T[name][0:8, lo:hi], name, lo, hi)
+
     def small(out, mats, rhs_name, n16):
         for b in range(16):
             mm(out, V(mats, sl(b * 128, b * 128 + 128)), V(rhs_name, sl(b, n16, 16)), b == 0, b == 15)
+
+    def spread(h16):
+        for b in range(16):
+            mm(V("PT", sl(256 + b, 512, 16)), V("Rr", sl(b * 128, b * 128 + 128)), V(h16), True, True)
 
     AND, SHR = A.bitwise_and, A.arith_shift_right
 
@@ -276,15 +311,13 @@ def rank_program(g, core, T, topo):
         dma("sp", "dln", 32, (T["LNI"][0:128:16, out_sl], "LNI", o[2], o[3]), (T[nm][:], nm, 0, 1))
     iota(V("im"), [[1, 128]])
     iota(V("ip"), [[0, 1]], 0, 1)
-    iota(V("LClo"), [[0, 16], [16, 16]])
-    iota(V("LChi"), [[256, 16], [0, 16]])
+    iota(V("LC"), [[16, 256]])
     iota(V("IC"), [[16, 16]])
+    iota(V("RF"), [[0, 16], [1, 16]])
     iota(V("II"), [[16, 16], [0, 16]])
     iota(V("POS0"), [[16, 16], [-256, 16]], 3840)
     iota(V("POS1"), [[256, 16], [16, 16]])
-    iota(V("RF"), [[0, 16], [1, 16]])
-    iota(V("WIN0", sl(0, 4368)), [[0, 4368]])
-    iota(V("J32"), [[16, 8], [0, 16], [1, 16]])
+    iota(V("WIN", sl(0, 4352)), [[0, 4352]])
     iota(V("Rlo"), [[0, 2048]])
 
     i_ = lambda k: V("ii", sl(k, k + 1))
@@ -307,11 +340,11 @@ def rank_program(g, core, T, topo):
     for nm, c, h in (("RV0", 5, 3), ("RV1", 5, 4), ("RS0", 6, 3), ("RS1", 6, 4)):
         ts(V(nm), V("im"), col(c), A.is_equal, col(h), A.mult)
     tt(col(8), col(8), col(7), A.subtract)
-    ts(V("NEG2"), V("im"), col(0), A.is_equal, -2.0, A.mult)
+    ts(V("NEGI"), V("im"), col(0), A.is_equal, -1.0, A.mult)
     ac(V("E"), V("X", sl(0, 2048)), F.Copy, 0.0)
     for k in range(8):
         ac(V("E", sl(16 * k, 2048, 129)), V("BO", sl(16 * k, 16 * k + 16)))
-    ac(V("Rhi"), V("X", sl(0, 2048)), F.Copy, 0.0)
+    dma("sp", "de8", 16, top8("E8", 0, 2048), (T["E"][0:128:16, :], "E", 0, 2048))
     for k in range(2):
         tc(V("HX", k, sl(0, 8), sl(0, 2), sl(0, 16)), V("VI", sl(256 * k, 256 * k + 256)))
 
@@ -324,52 +357,56 @@ def rank_program(g, core, T, topo):
             tc(V("HL", 2 * k + 1, sl(0, 8), sl(0, 2), sl(0, 16)), V("VL", h))
         for a in range(4):
             dma("sp", "pst", 64, (T["PD0"][32 * a:32 * a + 32, :], "PD0", 1024 * a, 1024 * a + 1024), V("HL", a, sl(0, 8), sl(0, 2), sl(0, 16)))
+
+    def to_window(name, sem, lo):
         for a in range(4):
-            dma("sp", "po0", 64, (T["WIN0"][a:128:16, 16:4112], "WIN0", 16, 4112), (T["PD0"][32 * a:32 * a + 32, :], "PD0", 1024 * a, 1024 * a + 1024))
+            dma("sp", sem, 64, (T["WIN"][a:128:16, lo:lo + 4096], "WIN", lo, lo + 4096), (T[name][32 * a:32 * a + 32, :], name, 1024 * a, 1024 * a + 1024))
+
+    def half(pz, k):
+        return V(pz, sl(4 * k, 4 * k + 4))
 
     for k, dst in enumerate(("VU", "CU")):
         pz = "PZ%d" % k
         for kap in range(2):
-            o = V(pz, 0, sl(kap * 128, kap * 128 + 128))
             for sw in range(2):
-                mm(o, V(("RV%d", "RS%d")[sw] % kap), V("HX", k, sl(0, 8), (kap, 1 - kap)[sw], sl(0, 16)), sw == 0, sw == 1)
+                mm(half(pz, kap), V(("RV%d", "RS%d")[sw] % kap), V("HX", k, sl(0, 8), (kap, 1 - kap)[sw], sl(0, 16)), sw == 0, sw == 1)
         for kap in range(2):
-            tc(V("FT", sl(0, 8), kap, sl(0, 16)), V(pz, 0, sl(kap * 128, kap * 128 + 128)))
-        tc(V("FIN"), V("FT", sl(0, 8), sl(0, 2), sl(0, 16)))
-        run("dve", lambda e: e.transpose(V("VMV")[0], V("FIN")[0]), [V("VMV")], [V("FIN")])
+            tc(V("FT", sl(0, 8), kap, sl(0, 16)), half(pz, kap))
+        run("dve", lambda e: e.transpose(V("VMV")[0], V("FT")[0]), [V("VMV")], [V("FT")])
         tc(V(dst), V("VMV"))
         if k == 0:
             tc(V("WV", sl(16, 272)), V("VMV"))
     fill(V("WV", sl(0, 16)), 0)
-    fill(V("Z", sl(0, 16), sl(0, 32)), 0.0)
-    fill(V("XV", sl(0, 16)), 0.0)
+    fill(V("Z", ALL, sl(0, 2)), 0.0)
 
     def consts_early():
         tc(col(9), V("WTI"))
         fill(V("RB"), 1.0)
         fill(V("RB", sl(0, 256, 16)), 0.0)
         fill(V("SEEDS"), 1.0)
+        fill(V("LC", sl(0, 256, 16)), 16777216.0)
+        fill(V("Q0N"), 0.0)
+        fill(V("Q0N", sl(0, 256, 16)), -8192.0)
         lengths_in()
         for _ in start_step(0):
             pass
-        fill(V("Q0T"), 0.0)
-        fill(V("Q0T", sl(0, 256, 16)), 16777216.0)
-        ts(V("LClo"), V("LClo"), col(1), A.add)
 
     def consts_mid():
         ts(V("PS", sl(256, 512)), V("RF"), col(1), A.is_gt)
+        ts(V("DM"), V("RF"), col(1), A.is_lt)
+        ts(V("SDM"), V("RF"), col(1), A.is_lt, -1.0, A.add)
         tc(V("RF"), V("RB"))
-        ts(V("NEGI"), V("im"), col(0), A.is_equal, -1.0, A.mult)
+        fill(V("DM", sl(0, 256, 16)), 0.0)
+        ts(V("ID2"), V("im"), col(0), A.is_equal, 2.0, A.mult)
+        ts(V("NEGH"), V("im"), col(0), A.is_equal, -0.5, A.mult)
+        ts(col(12), col(1), -16.0, A.add)
         fill(V("SEEDP"), -1.0)
-        fill(V("SEEDP", sl(1, 256, 16)), -65.0)
+        fill(V("SEEDP", sl(1, 256, 16)), 63.0)
         for nm in ("POS0", "POS1", "II", "IC"):
             ts(V(nm), V(nm), col(1), A.add)
         ts(V("D01"), V("im"), col(0), A.is_equal, col(7), A.mult)
-        tt(col(10), col(0), col(0), A.subtract)
-        ts(col(10), col(10), 2.0, A.add, col(0), A.add)
+        ts(col(10), col(0), 2.0, A.add)
         ts(V("S23"), V("im"), col(10), A.is_equal, col(7), A.mult)
-        ts(V("NBm"), V("J32"), col(0), A.is_equal, -1.0, A.mult)
-        fill(V("Z2", sl(0, 16), sl(224, 256)), 0.0)
         ts(col(11), col(7), 2048.0, A.mult, col(8), A.add)
 
     def places(m, grow):
@@ -379,17 +416,23 @@ def rank_program(g, core, T, topo):
 
     def consts_late():
         ts(V("DD"), V("IC"), 2048.0, A.add)
-        places(0, -256.0)
-        fill(V("SEEDG"), -1.0)
-        fill(V("SEEDG", sl(1, 256, 16)), -65.0)
         ts(V("t1"), V("im", sl(0, 16)), col(1), A.is_equal)
         for b in range(16):
             ts(V("Rr", sl(128 * b, 128 * b + 128)), V("BO"), V("t1", sl(b, b + 1)), A.mult)
+        places(0, -256.0)
+        fill(V("SEEDG"), -1.0)
+        fill(V("SEEDG", sl(1, 256, 16)), -65.0)
+        ts(V("G8"), V("G8"), col(2), A.is_equal, 4096.0, A.mult)
+        ts(i_(4), V("ip"), 3, SHR, 1, AND)
+        tc(col(13), i_(4))
+        ts(V("OFG"), V("i8"), col(13), A.add)
 
     def consts_last():
-        fill(V("SEEDN"), -0.0625)
-        fill(V("SEEDN", sl(1, 256, 16)), 3.9375)
         places(1, 16.0)
+        ts(V("IDK"), V("im"), col(0), A.is_equal, 4096.0, A.mult)
+        ts(V("DD1"), V("DD"), 1.0, A.add)
+        ts(col(14), col(1), 0.5, A.is_gt)
+        ts(col(15), col(14), -1.0, A.add)
 
     def lengths_in():
         tc(V("LNB", sl(0, 256)), V("LNI", sl(0, 256)))
@@ -412,59 +455,38 @@ def rank_program(g, core, T, topo):
         yield ts(V("M1"), V("NS"), 3.0, A.is_lt, -16777216.0, A.mult)
         yield ts(V("M2"), V("NS"), 0.5, A.is_le, 8192.0, A.mult)
         yield tc(V("YM%d" % t, sl(256, 272)), V("LIVE"))
+        yield ts(V("R84"), V("LIVE"), -20.0, A.mult, -44.0, A.add)
+        yield ts(V("REST"), V("LIVE"), -1.0, A.mult, 1.0, A.add)
+        yield ts(V("NR"), V("LIVE"), 99.0, A.mult)
+        yield ts(V("HAS"), V("NN"), 0.5, A.is_ge)
+        yield ts(V("A0"), V("WV", sl(31, 272, 16)), 1.0, A.add)
+        yield tt(V("NR"), V("NR"), V("NN"), A.add)
 
-    def push(t, name, out_name, sem, via):
+    def push(t, name, k):
+        land, sem, via = SENT[k]
         dst = T.cores[(rank + 1 + t % 7) % len(T.cores)]
         rl = _relays(core, dst, topo)
-        to = rl[via] if rl else dst
-        before("g", [V(name)])
-        n_loc[0] += _send(core, T, topo, g, T[out_name][:], T[name][:], sem, to)
+        before("g", [V(name + str(t))])
+        n_loc[0] += _send(core, T, topo, g, T[land + str(t)][:], T[name + str(t)][:], sem + str(t), rl[via] if rl else dst)
         total["loc"] = n_loc[0]
 
-    def came(t, name, sem):
+    def came(t, k):
+        land, sem, via = SENT[k]
         src = T.cores[(rank - 1 - t % 7) % len(T.cores)]
         rl = _relays(src, core, topo)
-        arrive(name + str(t), sem + str(t), len(topo.engines(rl[0] if rl else src, core)[:8]))
-
-    def dedupe(vict, val1, act, vald, off, cb, meanwhile):
-        tt(V("HE"), val1, act, A.mult)
-        mm(V("PT", sl(256, 512)), V("BO"), V("ZERO"), True, False)
-        for c in range(16):
-            ts(V("EQ", c, sl(0, 256 - 16 * c)), V(vict, sl(16 * c, 256)), V("HE", sl(c, c + 1)), A.is_equal)
-            if c < 15:
-                mm(V("PT", sl(272 + 16 * c, 512)), V("BO"), V("EQ", c, sl(16, 256 - 16 * c)), False, False)
-        d = V("EQ", sl(0, 16), sl(0, 16))
-        tt(V("Te"), vald, act, A.mult)
-        tt(d, d, V("PS", sl(256, 512)), A.mult)
-        if cb != "act":
-            lists_in(0)
-        mm(V("PT", sl(256, 512)), V("BO"), d, False, True)
-        if cb != "act":
-            lists_in(1)
-            if mid[0]:
-                mid[0]()
-                mid[0] = None
-        if cb == "act":
-            ac(V("CB"), V("PT", sl(256, 512)))
-        else:
-            tc(V("CB"), V("PT", sl(256, 512)))
-        small(V("PS", sl(32, 48)), "E", "CB", 256)
-        meanwhile()
-        yield ts(V("Td"), V("PS", sl(32, 48)), 0.5, A.is_lt)
-        yield tt(V("Td"), V("Td"), V("Te"), A.mult)
-        yield tt(V("t1"), V("Td"), V("DD"), A.add)
-        yield tc(V(off), V("t1"))
+        arrive(land + str(t), sem + str(t), len(topo.engines(rl[via] if rl else src, core)[:8]))
 
     def lists_in(j):
-        nxt = now[0]
         for b in range(16):
-            mm(V("PZ3" if j > 1 else "PZ0", 0, sl(64 * j, 64 * j + 64)), V("Ec", sl(b * 128, b * 128 + 128)), V(nxt, sl(16 + 1024 * j + b, 1040 + 1024 * j, 16)), b == 0, b == 15)
-
-    now, mid = [None], [None]
+            if j < 2:
+                o, r = V("PZ3", sl(4 * j, 4 * j + 4), sl(0, 2), sl(0, 13)), V("NLa", sl(1664 * j + b, 1664 * j + 1664, 16))
+            else:
+                o, r = V("PZ3", sl(0, 8), sl(0, 2), sl(13, 16)), V("NLb", sl(b, 768, 16))
+            mm(o, V("Ec", sl(b * 128, b * 128 + 128)), r, b == 0, b == 15)
 
     def unpack(k):
         h = sl(128 * k, 128 * k + 128)
-        w = V(("PZ0", "PZ3")[k], 0, h)
+        w = half("PZ3", k)
         hv = V("WV", sl(h.start + 16, h.stop + 16))
         yield ts(hv, w, 2.0 ** -11, A.mult, -0.49976, A.add)
         yield tc(V("WC", h), w)
@@ -472,288 +494,324 @@ def rank_program(g, core, T, topo):
         yield ts(V("WC", h), V("WC", h), 2047, AND)
         yield tc(V("CU", h), V("WC", h))
 
+    def both(a, b):
+        for _ in a:
+            next(b, None)
+        for _ in b:
+            pass
+
     for t in range(ST):
-        cur, nxt = "WIN%d" % (t % 2), "WIN%d" % (1 - t % 2)
         md = min(t, 1)
         unit = (256.0, -16.0)[md]
         S = str(t)
-        ym, sm = "YM" + S, "SM" + S
+        ym, sm, km = "YM" + S, "SM" + S, "KM" + S
 
-        def gv(u, n):
-            gather("dve", V("XV", sl(16 + 512 * u, 16 + 512 * u + 512 * n)), V("X", *X_WIN), V("VU", sl(32 * u, 32 * u + 32 * n)))
+        def gv(q, u):
+            gather(q, V("XV", sl(512 * u, 512 * u + 512)), V("X", *X_WIN), V("VU", sl(32 * u, 32 * u + 32)), 0.5)
 
-        def gc(q, u, n):
-            gather(q, V("XC", sl(512 * u, 512 * u + 512 * n)), V("X", *X_WIN), V("CU", sl(32 * u, 32 * u + 32 * n)))
+        def gc(u):
+            for c in (2 * u, 2 * u + 1):
+                q0 = 2 * md
+                off = V("CU", sl(16 * c + q0, 16 * c + 16))
+                h = sl(256 * c + 16 * q0, 256 * c + 256)
+                tt(V("XC", h), at(V("X", *X_WIN), off), V("XV", h), A.subtract, [off])
 
         def bend(u):
             pz = "PZ%d" % (u % 4)
             for k in range(2):
-                o = (2 * u + k) * 256
-                for src, mat, a in (("XV", "ID", 16 + o + 32), ("XV", "ID", o + 32), ("XC", "NEG2", o + 32)):
-                    mm(V(pz, k, sl(32, 256)), V(mat), V(src, sl(a, a + 224)), a == 16 + o + 32, src == "XC")
-            ac(V("Z", sl(2 * u, 2 * u + 2), sl(32, 256)), V(pz, sl(0, 2), sl(32, 256)), F.Abs, 4096.0)
+                o = V(pz, sl(7 * k, 7 * k + 7))
+                a = 256 * (2 * u + k)
+                mm(o, V("ID"), V("XV", sl(a + 16, a + 240)), True, False)
+                mm(o, V("NEGI"), V("XC", sl(a + 32, a + 256)), False, True)
 
-        def key(j):
-            o = V("PK", sl(64 * j, 64 * j + 64))
-            for k, m in enumerate(("M1", "Q0T", "LChi", "LClo")):
-                mm(o, V("ID"), V(m, sl(64 * j, 64 * j + 64)), k == 0, False)
+        def babs(u):
+            ac(V("Z", sl(2 * u, 2 * u + 2), sl(2, 16)), V("PZ%d" % (u % 4), sl(0, 14)), F.Abs, 8192.0)
+
+        def key(c0, c1):
+            if c1 == 16:
+                for h in (sl(0, 16 * c0), sl(16 * c0, 256)):
+                    mm(V("PK", h), V("ID"), V("M1", h), False, False)
+                    mm(V("PK", h), V("ID"), V("LC", h), False, False)
             for b in range(16):
-                mm(o, V("E", sl(b * 128, b * 128 + 128)), V("Z", sl(4 * j, 4 * j + 4), sl(b, 256, 16)), False, b == 15)
+                mm(V("PK", sl(16 * c0, 16 * c1)), V("E", sl(b * 128, b * 128 + 128)), V("Z", sl(c0, c1), ALL, b), b == 0 and c0 == 0, b == 15 and c1 == 16)
+
+        banks = ((0, 16, 12, 2), (0, 8, 8, 4), (8, 8, 8, 4), (0, 8, 4, 4), (8, 8, 4, 4), (0, 8, 0, 4), (8, 8, 0, 4))
+
+        def dist_x(v):
+            c0, nc, q0, nq = banks[v]
+            for c in range(nc):
+                a = 256 * (c0 + c) + 16 * q0
+                mm(V("PZ%d" % (v % 4), sl(c * nq // 2, (c + 1) * nq // 2)), V("ID"), V("XV", sl(a, a + 16 * nq)), c == 0, False)
+
+        def dist_y(v):
+            c0, nc, q0, nq = banks[v]
+            pz = "PZ%d" % (v % 4)
+            for k in range(nq):
+                mm(V(pz, sl(k // 2, 16, nq // 2), k % 2), V("NEGH"), V(ym, sl(16 * c0, 16 * (c0 + nc))), False, k == nq - 1)
+            ac(V("Z2", sl(c0, c0 + nc), sl(q0, q0 + nq)), V(pz), F.Abs, 2.0)
+
+        def dist_sum(q0, q1):
+            if q1 == 14:
+                mm(V("PQ", ALL, ALL), V("ID"), V("PRE"), False, False)
+            for b in range(16):
+                mm(V("PQ", ALL, sl(q0, q1)), V("E", sl(b * 128, b * 128 + 128)), V("Z2", ALL, sl(q0, q1), b), False, b == 15 and q0 == 0)
 
         if t:
-            for a in range(4):
-                dma("sp", "po" + S, 64, (T["PD" + S][32 * a:32 * a + 32, :], "PD" + S, 1024 * a, 1024 * a + 1024), (T[cur][a:128:16, 16:4112], cur, 16, 4112))
-            push(t, "PD" + S, "PI" + S, "am" + S, 0)
+            for nl, lo, hi in (("NLa", 0, 208), ("NLb", 208, 256)):
+                for a in range(4):
+                    dma("sp", "po" + S, 128, (T["PD" + S][32 * a:32 * a + 32, :, lo:hi], "PD" + S, 1024 * a, 1024 * a + 1024), (T[nl][a:128:16, :], nl, 0, 4096))
+            push(t, "PD", 0)
+            to_window("PD" + S, "pw" + S, 0)
         else:
             iota(V("SHS"), [[0, 256]])
-            iota(V("ZERO"), [[0, 256]])
+            iota(V("G8"), [[0, 16], [1, 8]])
+            iota(V("i8"), [[2, 8]])
             iota(V("ONES"), [[0, 128]], 1)
             iota(V("N192"), [[0, 256]], -192)
-            iota(V("WIN1", sl(0, 16)), [[0, 16]])
-        gv(0, 1)
-        gv(1, 1)
+        gv("dve", 0)
+        gv("act", 1)
+        gc(0)
+        bend(0)
+        gv("act", 2)
+        if t:
+            for _ in unpack(1):
+                pass
+        gv("act", 3)
+        gc(1)
+        bend(1)
+        babs(0)
         if t == 0:
             payload_in()
-            push(t, "PD" + S, "PI" + S, "am" + S, 0)
-        gc("act", 0, 1)
-        gc("act", 1, 1)
-        gc("act", 2, 2)
-        gv(2, 2)
-        bend(0)
-        bend(1)
+            push(t, "PD", 0)
+            to_window("PD0", "pw0", 0)
+        gv("act", 4)
+        babs(1)
+        gc(2)
         bend(2)
+        gv("act", 5)
+        gc(3)
+        bend(3)
+        babs(2)
+        gv("act", 6)
+        gc(4)
+        bend(4)
+        babs(3)
+        gc(5)
+        bend(5)
+        key(0, 8)
+        gv("act", 7)
+        babs(4)
+        gc(6)
+        bend(6)
+        babs(5)
+        gc(7)
+        key(8, 12)
+        bend(7)
+        babs(6)
+        babs(7)
         if t == 0:
             consts_early()
-        else:
-            st = start_step(t)
-            for _ in unpack(1):
-                next(st)
-            for _ in st:
-                pass
-        gc("act", 4, 2)
-        gv(4, 2)
-        bend(3)
-        gc("act", 6, 1)
-        key(0)
-        gv(6, 2)
-        bend(4)
-        bend(5)
-        key(1)
-        gc("dve" if t else "act", 7, 1)
-        bend(6)
-        bend(7)
-        key(2)
-        if t == 0:
             ac(V("wE"), V("E"), F.Copy, col(9))
             consts_mid()
-
-        def dist_x(u):
-            mm(V("PZ%d" % (u % 4), sl(0, 2), sl(0, 256)), V("ID"), V("XV", sl(16 + 512 * u, 528 + 512 * u)), True, False)
-
-        def dist_y(u):
-            pz = "PZ%d" % (u % 4)
-            for k in range(2):
-                c = 2 * u + k
-                mm(V(pz, k, sl(0, 224)), V("YT", sl(128 * (c // 8), 128 * (c // 8) + 128)), V("NBm", sl(256 * (c % 8), 256 * (c % 8) + 224)), False, k == 1)
-            ac(V("Z2", sl(2 * u, 2 * u + 2), sl(0, 224)), V(pz, sl(0, 2), sl(0, 224)), F.Abs)
-
-        def dist_sum(j):
-            o = V("PQ", sl(64 * j, 64 * j + 64))
-            mm(o, V("ID"), V("M2", sl(64 * j, 64 * j + 64)), True, False)
-            mm(o, V("ID"), V("PRE", sl(64 * j, 64 * j + 64)), False, False)
-            for b in range(16):
-                mm(o, V("E", sl(b * 128, b * 128 + 128)), V("Z2", sl(4 * j, 4 * j + 4), sl(b, 256, 16)), False, b == 15)
-
+        else:
+            for _ in start_step(t):
+                pass
         dist_x(0)
         dist_x(1)
+        key(12, 16)
+        mm(V("PQ", ALL, ALL), V("ID"), V("M2"), True, False)
+        mm(V("PQ", ALL, ALL), V("ID"), V("Q0N"), False, False)
         dist_x(2)
-        key(3)
         dist_x(3)
         scan(V("KM"), V("RF"), V("PK", sl(0, 256)), A.mult, A.max)
         tc(V("KI"), V("KM", sl(15, 256, 16)))
         ts(V("OFI"), V("KI"), 4095, AND)
-        tc(V("OFU"), V("OFI"))
-        gather("act", V("G3"), V("XC", sl(0, 4096)), V("OFU"))
-        gather("dve", V("G1"), V("XV", sl(16, 4112)), V("OFU"))
-        gather("dve", V("G2"), V("XV", sl(0, 4096)), V("OFU"))
-        yy = (("G1", "ID"), ("G3", "NEGI"), ("G2", "ID"))
-        for h in range(2):
-            for k, (gm, mat) in enumerate(yy):
-                mm(V("PT", sl(256 + 128 * h, 384 + 128 * h)), V(gm, sl(128 * h, 128 * h + 128)), V(mat), k == 0, k == 2)
-        ts(V("QK"), V("OFI"), 4, SHR, 15, AND)
-        ts(V("YT"), V("PT", sl(256, 512)), 0.0, A.max, 63.0, A.min)
-        for u in range(4):
-            dist_y(u)
-        for k, (gm, mat) in enumerate(yy):
+        ts(V("OFU"), V("OFI"), col(1), A.add)
+        ts(V("OFN"), V("OFI"), col(12), A.add)
+        gather("act", V("G3"), V("XC"), V("OFU"))
+        gather("dve", V("G1"), V("XV"), V("OFU"))
+        gather("dve", V("G2"), V("XV"), V("OFN"))
+        for k, (gm, mat) in enumerate((("G1", "ID"), ("G3", "NEGI"), ("G2", "ID2"))):
             mm(V("PT", sl(0, 256)), V(mat), V(gm), k == 0, k == 2)
+        ts(V("QK"), V("OFI"), 4, SHR, 15, AND)
         ts(V(ym, sl(0, 256)), V("PT", sl(0, 256)), 0.0, A.max, 63.0, A.min)
-        push(t, ym, "YR" + S, "ay" + S, 1)
+        dist_y(0)
+        small(V("PS", sl(16, 32)), "wE", ym, 256)
+        for v in range(1, 4):
+            dist_y(v)
+        push(t, "YM", 1)
         if t == 0:
-            iota(V("WIN0", sl(4368, 8208)), [[0, 3840]])
-        ts(V("SEEDP", sl(0, 256, 16)), V("QK"), 64.0, A.add)
+            iota(V("WIN", sl(4352, 8192)), [[0, 3840]])
+        tt(V("SEEDP", sl(0, 256, 16)), V("QK"), V("R84"), A.add)
         scan(V("SK"), V("RB"), V("SEEDP"), A.mult, A.add)
+        p0 = V("PK", sl(0, 256))
+        ts(V(km, sl(0, 16)), V("QK"), -unit, A.mult, 4096.0 + 16.0 * unit, A.add)
+        ts(p0, V("SK"), 0.0, A.is_equal)
         ts(V("PRE"), V("SK"), 1.5, A.is_le, 8192.0, A.mult)
+        tt(V("VKS"), p0, V("WV", sl(16, 272)), A.mult)
+        tc(V("UI"), V("PS", sl(16, 32)))
+        scan(V("VKT"), V("RF"), V("VKS"), A.mult, A.add)
+        ts(V("UI"), V("UI"), 2047, AND)
+        tt(V("VNS"), p0, V("WV", sl(15, 271)), A.mult)
+        tt(V("SQ"), V("UI"), V("UI"), A.mult)
+        ts(V("Td"), V("VKT", sl(15, 256, 16)), 37.0, A.mult)
+        ts(V("SQ"), V("SQ"), 5, SHR)
+        scan(V("VNT"), V("RF"), V("VNS"), A.mult, A.add)
+        tt(V("HI"), V("SQ"), V("Td"), A.add)
+        ts(V("QM"), V("QK"), -16.0, A.add)
+        ts(V("HI"), V("HI"), 2047, AND)
+        ts(V(km, sl(16, 32)), V("VNT", sl(15, 256, 16)), 1.0, A.add)
+        tc(V("H16"), V("HI"))
+        push(t, "KM", 2)
         if t == 0:
             ts(V("OF0"), V("QK"), -256.0, A.mult, 3840.0, A.add)
             tt(V("Ta"), V("OF0"), V("IC"), A.add)
             tc(V("OFP"), V("Ta"))
-        off = ("OFP", "OFU")[md]
-        if t == 0:
             consts_late()
-        dist_x(4)
-        dist_y(4)
-        dist_x(5)
-        dist_y(5)
+        off = ("OFP", "OFU")[md]
+        for v in range(4, 7):
+            dist_x(v)
+            dist_y(v)
+            if v == 5:
+                spread("H16")
+        dist_sum(8, 14)
+        dist_sum(4, 8)
         if t == 0:
+            ac(V("Rhi"), V("X", sl(0, 2048)), F.Copy, 0.0)
             for k in range(8):
                 ac(V("Rhi", sl(16 * k, 2048, 128)), V("ID", sl(16 * k, 16 * k + 16)))
                 ac(V("Rlo", sl(16 * k + 1, 2048, 128)), V("ID", sl(16 * k, 16 * k + 16)))
-        small(V("PS", sl(16, 32)), "wE", ym, 256)
-        dist_sum(0)
-        p0 = V("PK", sl(0, 256))
-        ts(p0, V("SK"), 0.0, A.is_equal)
-        ts(V("QM"), V("QK"), -16.0, A.add)
-        tt(V("VKS"), p0, V("WV", sl(16, 272)), A.mult)
-        tt(V("VNS"), p0, V("WV", sl(15, 271)), A.mult)
-        scan(V("VKT"), V("RF"), V("VKS"), A.mult, A.add)
-        scan(V("VNT"), V("RF"), V("VNS"), A.mult, A.add)
+        gather("act", V("PG1"), V("WIN", sl(0, 4096)), V(off))
+        gather("act", V("PG2"), V("WIN", (sl(256, 4352), sl(0, 4096))[md]), V(("OFP", "OFN")[md]))
+        dist_sum(0, 4)
+        tc(V("HG"), V("HI"))
         tt(V("OHT"), p0, V("TPk%d" % md), A.mult)
-        tc(V(sm, sl(32, 48)), V("VNT", sl(15, 256, 16)))
-        ts(V(sm, sl(16, 32)), V("QK"), -unit, A.mult, 4096.0 + 16.0 * unit, A.add)
-        tc(V("UI"), V("PS", sl(16, 32)))
-        ts(V("Td"), V("VKT", sl(15, 256, 16)), 37.0, A.mult)
-        ts(V("UI"), V("UI"), 2047, AND)
-        tt(V("SQ"), V("UI"), V("UI"), A.mult)
-        ts(V("SQ"), V("SQ"), 5, SHR)
-        tt(V("HI"), V("SQ"), V("Td"), A.add)
-        ts(V("HI"), V("HI"), 2047, AND)
         ts(V("HP", sl(0, 16)), V("HI"), 1792, AND)
         ts(V("HP", sl(16, 32)), V("HI"), 255, AND)
+        ts(V("GT"), V("SK"), 0.5, A.is_gt)
         tc(V("HHL"), V("HP"))
-        tc(V("H16"), V("HI"))
-        tc(V("HF"), V("HI"))
-        ts(V("HG"), V("HF"), 1.0, A.add)
-        tt(V("HD"), V("HF"), V("DD"), A.subtract)
-        dist_x(6)
-        dist_y(6)
-        dist_sum(1)
-        dist_x(7)
-        dist_y(7)
-        gather("act", V("PG1"), V(cur, sl(16, 4112)), V(off))
-        gather("act", V("PG2"), V(cur, (sl(272, 4368), sl(0, 4096))[md]), V(off))
-        dist_sum(2)
-        dist_sum(3)
-        for b in range(16):
-            mm(V("PT", sl(b, 256, 16)), V("Rr", sl(b * 128, b * 128 + 128)), V("H16"), True, True)
+        tt(V("OHPP"), V("OHT"), V("POS%d" % md), A.add)
+        tc(V("HR"), V("PT", sl(256, 512)))
+        for c in range(16):
+            ts(V("EQ", c, sl(0, 256 - 16 * c)), V("HR", sl(16 * c, 256)), V("HG", sl(c, c + 1)), A.is_equal)
+        d = V("EQ", ALL, ALL)
+        tt(d, d, V("PS", sl(256, 512)), A.mult)
         ex = V("PK", sl(0, 256))
         mm(ex, V("D01"), V("PG1"), True, False)
         mm(ex, V("S23"), V("PG2"), False, True)
-        ph = V("PQ", sl(256, 512))
-        o = V("PK", sl(256, 512))
-        mm(o, V("S23"), V("PG1"), True, False)
+        mm(V("PK", sl(256, 512)), V("S23"), V("PG1"), True, False)
         for b in range(16):
             for k, mat in enumerate(("Rhi", "Rlo")):
                 mm(V("PK", sl(256 + b, 512, 16)), V(mat, sl(b * 128, b * 128 + 128)), V("HHL", sl(16 * k, 16 * k + 16)), False, b == 15 and k == 1)
-        ac(V(cur, sl(8208, 8720)), V("PK", sl(0, 512)))
+        ac(V("WIN", sl(8192, 8704)), V("PK"))
         if t == 0:
             ac(V("Ec"), V("E"), F.Copy, col(11))
-        ts(V("NF"), V("PQ", sl(0, 256)), V("lim"), A.is_gt)
+        ts(V("NF"), V("PQ", ALL, ALL), V("lim"), A.is_gt)
         scan(V("MS"), V("NF"), V("NF"), A.mult, A.add)
         M = V("MS", sl(15, 256, 16))
         ts(V("CL"), M, 15.5, A.is_le)
         tt(V("Ta"), M, V("QM"), A.add)
-        SZ = V(sm, sl(0, 16))
-        tt(SZ, V("Ta"), V("CL"), A.mult)
-        push(t, sm, "SR" + S, "as" + S, 1)
         tt(V("GR"), V("LIVE"), V("CL"), A.subtract)
-        ts(V("HR"), V("PT", sl(0, 256)), 1.0, A.add)
-
-        def own():
-            ts(V("Tb"), V("GR"), -256.0, A.mult, 320.0, A.add)
-            tt(V("SEEDG", sl(0, 256, 16)), V("Tb"), V("QK"), A.add)
-            tt(V("Ta"), SZ, V("GR"), A.subtract)
-            scan(V("OHG"), V("RB"), V("SEEDG"), A.mult, A.add)
-            ts(V("Tb"), V("Ta"), unit, A.mult)
-            ts(V("NR"), V("LIVE"), 99.0, A.mult)
-            ts(ph, V("OHG"), 1.0, A.is_equal)
-            tt(V("OHPP"), V("OHT"), V("POS%d" % md), A.add)
-            tt(V("NR"), V("NR"), V("NN"), A.add)
-            ts(V("QN"), V("QK"), 0.0625, A.mult, -4.0, A.add)
-
-            run("dve", lambda e: e.tensor_reduce(V("cls")[0], V("CL")[0], AxisListType.X, A.add), [V("cls")], [V("CL")])
-            tc(V("CLB"), V("cls"))
-            mm(V("PS", sl(64, 65)), V("ONES"), V("CLB"), True, True)
-
-        dd = dedupe("HR", V("HG"), V("GR"), V("HD"), "OFH", "act", own)
-        next(dd)
+        SZ = V(sm)
+        tt(SZ, V("Ta"), V("CL"), A.mult)
+        push(t, "SM", 3)
+        tt(V("STA"), at(V("GR"), V("OFG")), V("G8"), A.mult, [V("OFG")])
+        ts(V("NG"), V("GR"), -4096.0, A.mult, 4096.0, A.add)
+        for c in range(16):
+            mm(top8("PT", 16 * c, 256), V("STA", sl(8 * c, 8 * c + 8)), V("EQ", c, sl(0, 256 - 16 * c)), c == 0, c == 15)
+        oh = V("PS", sl(32, 48))
+        mm(oh, V("ID"), V("H16"), True, False)
+        mm(oh, V("ID"), V("NG"), False, False)
+        ph = V("PQ", ALL, sl(16, 32))
+        for k in range(3):
+            came(t, k)
+        to_window("PI" + S, "pi" + S, 4096)
+        ts(V("Tb"), V("GR"), -256.0, A.mult, 320.0, A.add)
+        tt(V("Ta"), SZ, V("GR"), A.subtract)
+        tt(V("SEEDG", sl(0, 256, 16)), V("Tb"), V("QK"), A.add)
+        ts(V("Ta"), V("Ta"), unit, A.mult)
+        tt(V("RS"), V("KR" + S, ALL), V("REST"), A.mult)
+        scan(V("OHG"), V("RB"), V("SEEDG"), A.mult, A.add)
+        tt(V("SHS", sl(0, 256, 16)), V("Ta"), V("RS"), A.add)
+        ts(ph, V("OHG"), 1.0, A.is_equal)
+        run("dve", lambda e: e.tensor_reduce(V("cls")[0], V("CL")[0], AxisListType.X, A.add), [V("cls")], [V("CL")])
         tt(ph, ph, V("TPn%d" % md), A.mult)
+        tc(V("CLB"), V("cls"))
+        tt(ph, ph, V("OHPP"), A.add)
+        cb = top8("CB", 0, 256)
+        tc(cb, top8("PT", 0, 256))
+        for b in range(16):
+            box, a = PLACE["CB"]
+            mm(oh, top8("E8", 128 * b, 128 * b + 128), (T[box][0:8, a + b:a + 256:16],) + cb[1:], False, b == 15)
+        scan(V("SHF"), V("GT"), V("SHS"), A.mult, A.add)
+        tt(V("HAS"), V("HAS"), V("YR" + S, sl(256, 272)), A.mult)
+        tt(V("SRC"), ph, V("SHF"), A.add)
+        tt(V("A0"), V("A0"), V("HAS"), A.mult)
+        ts(V("SRCU"), V("SRC", ALL, sl(0, 13)), 8703.0, A.min)
+        tt(V("DAB"), V("KR" + S, sl(16, 32)), V("A0"), A.subtract)
+
+        def early(c0, c1):
+            gather("act", V("NLa", sl(208 * c0, 208 * c1)), V("WIN"), V("SRCU", sl(13 * c0, 13 * c1)))
+
+        early(0, 8)
+        early(8, 12)
+        tt(V("t1"), oh, V("DD"), A.min)
         tt(V("NN"), V("NN"), V("GR"), A.add)
-        next(dd)
-        tt(V("OHPP"), ph, V("OHPP"), A.add)
-        tc(V("ci"), V("PS", sl(64, 65)))
+        tc(V("OFH"), V("t1"))
         ts(V("NN"), V("NN"), 16.0, A.min)
+        mm(V("PS", sl(64, 65)), V("ONES"), V("CLB"), True, True)
         xw = V("X", *X_ALL)
-        put = lambda: run("dve", lambda e: e.tensor_copy(xw[0].indirect(V("OFH")[0]), T[ym][:, 0:256]), [xw], [V("OFH"), V(ym, sl(0, 256))])
-        ts(V("ci"), V("ci"), 31, AND)
+        run("dve", lambda e: e.tensor_copy(at(xw, V("OFH"))[0], T[ym][:, 0:256]), [xw], [V("OFH"), V(ym, sl(0, 256))])
         tt(V("NN"), V("NN"), SZ, A.subtract)
+        tc(V("ci"), V("PS", sl(64, 65)))
         if t == 0:
             consts_last()
-        came(t, "PI", "am")
-        came(t, "YR", "ay")
-        came(t, "SR", "as")
-        if t == 0:
-            iota(V("WIN1", sl(4112, 8208)), [[0, 4096]])
-        for a in range(4):
-            dma("sp", "pi" + S, 64, (T[cur][a:128:16, 4112:8208], cur, 4112, 8208), (T["PI" + S][32 * a:32 * a + 32, :], "PI" + S, 1024 * a, 1024 * a + 1024))
-        sr = V("SR" + S, sl(0, 16))
+        ts(V("ci"), V("ci"), 31, AND)
+        came(t, 3)
+        sr = V("SR" + S)
         tt(V("TK"), sr, V("NR"), A.is_gt)
-        v0 = V("WV", sl(31, 272, 16))
-        tt(V("Tc"), V("SR" + S, sl(32, 48)), v0, A.subtract)
-        next(dd)
-        tt(V("SEEDN", sl(0, 256, 16)), V("QN"), V("TK"), A.add)
-        tt(V("Tc"), V("Tc"), V("TK"), A.mult)
-        tt(V("Ta"), V("SR" + S, sl(16, 32)), V("TK"), A.mult)
-        scan(V("SK"), V("RB"), V("SEEDN"), A.mult, A.add)
-        tt(V("VF"), v0, V("Tc"), A.add)
-        tt(V("SHS", sl(0, 256, 16)), V("Ta"), V("Tb"), A.add)
-        ts(V("GT"), V("SK"), 0.03, A.is_gt)
-        tc(V("H16"), V("VF"))
-        scan(ph, V("GT"), V("SHS"), A.mult, A.add)
+        tt(V("NT"), sr, V("NR"), A.is_le)
+        tt(V("Tc"), V("DAB"), V("TK"), A.mult)
+        tt(V("NT"), V("NT"), V("RS"), A.mult)
+        tt(V("V16"), V("Tc"), V("A0"), A.add)
+        spread("V16")
+        lists_in(0)
+        for k in range(3):
+            tt(V("SRT", ALL, k), V("SRC", ALL, 13 + k), V("NT"), A.subtract)
+        tt(V("HE"), V("Tc"), V("A0"), A.add)
+        ts(V("SRCL"), V("SRT"), 8703.0, A.min)
+        gather("act", V("NLb"), V("WIN"), V("SRCL"))
+        early(12, 16)
+        ts(V("SDM", sl(0, 256, 16)), V("HE"), col(14), A.mult, col(15), A.add)
+        ts(V("V0U"), V("HE"), -1.0, A.add)
+        scan(V("HEM"), V("DM"), V("SDM"), A.mult, A.add)
+        ts(V("NH"), V("HE"), 0.5, A.is_lt)
+        tc(V("VR"), V("PT", sl(256, 512)))
+        tt(V("EQD"), V("PT", sl(256, 512)), V("HEM"), A.is_equal)
+        mm(V("PK", sl(0, 256)), V("IDK"), V("EQD"), True, False)
+        mm(V("PK", sl(0, 256, 16)), V("ID"), V("V16"), False, False)
+        mm(V("PK", sl(0, 256, 16)), V("IDK"), V("NH"), False, False)
+        for c in range(15, 0, -1):
+            ts(V("EV", c, sl(0, 16 * c)), V("VR", sl(0, 16 * c)), V("HE", sl(c, c + 1)), A.is_equal)
+            mm(V("PK", sl(16 * c, 256)), V("IDK"), V("EV", sl(c, 16), sl(16 * c - 16, 16 * c)), False, c == 1)
+        tt(V("BS"), at(V("X", *X_WIN), V("V0U")), V("YR" + S, sl(0, 256)), A.add, [V("V0U")])
+        lists_in(2)
+        scan(V("OFS"), V("RF"), V("PK", sl(0, 256)), A.mult, A.add)
+        ts(V("BT"), V("BS"), 0.5, A.mult, 191.75, A.add)
+        tt(V("t1"), V("OFS", sl(15, 256, 16)), V("DD1"), A.min)
         tt(V("Ta"), sr, V("NN"), A.subtract)
-        next(dd)
-        tt(V("SRC"), V("OHPP"), ph, A.add)
-        tt(V("Ta"), V("Ta"), V("TK"), A.mult)
-        ts(V("VG"), V("VF"), 1.0, A.add)
-        ts(V("SRCU"), V("SRC"), 8703.0, A.min)
-        tt(V("NN"), V("NN"), V("Ta"), A.add)
-        tt(V("HD"), V("VF"), V("DD"), A.subtract)
-        tc(V("V0U"), V("VF"))
-        ts(V("HAS"), V("NN"), 0.5, A.is_ge)
-        win = V(cur, sl(16, 8720))
-        for b in range(16):
-            mm(V("PT", sl(b, 256, 16)), V("Rr", sl(b * 128, b * 128 + 128)), V("H16"), True, True)
-        for j in range(4):
-            gather("act", V(nxt, sl(16 + 1024 * j, 1040 + 1024 * j)), win, V("SRCU", sl(64 * j, 64 * j + 64)))
-        tt(V("HAS"), V("HAS"), V("YR" + S, sl(256, 272)), A.mult)
-        ts(V("VR"), V("PT", sl(0, 256)), 1.0, A.add)
-        tt(V("lim"), V("ci"), V("thc"), A.add)
-        mid[0] = put
+        ts(V("OFB"), V("t1"), -1.0, A.add)
+        tt(at(xw, V("OFB")), V("BT"), V("N192"), A.add, [V("OFB")])
 
-        now[0] = nxt
+        def lengths():
+            yield tt(V("lim"), V("ci"), V("thc"), A.add)
+            yield tt(V("Ta"), V("Ta"), V("TK"), A.mult)
+            yield tt(V("NN"), V("NN"), V("Ta"), A.add)
 
-        def blend_in():
-            run("dve", lambda e: e.tensor_tensor(V("BS")[0], T["X"][:, 0:2048].indirect(V("V0U")[0]), T["YR" + S][:, 0:256], A.add),
-                [V("BS")], [V("X", *X_WIN), V("V0U"), V("YR" + S, sl(0, 256))])
-            ts(V("BT"), V("BS"), 0.5, A.mult, 191.75, A.add)
-
-        dd = dedupe("VR", V("VG"), V("HAS"), V("HD"), "OFB", "dve", blend_in)
-        next(dd)
-        for _ in unpack(0):
-            next(dd, None)
-        run("dve", lambda e: e.tensor_tensor(xw[0].indirect(V("OFB")[0]), V("BT")[0], V("N192")[0], A.add),
-            [xw], [V("OFB"), V("BT"), V("N192")])
-        for j in range(2, 4):
-            lists_in(j)
+        both(unpack(0), lengths())
+        lists_in(1)
+    for _ in unpack(1):
+        pass
     dma("sp", "dout", 64, (T["yx"][:], "yx", 0, 1), V("X", sl(0, 2048)))
     for k, nm in enumerate(("RV0", "RV1", "RS0", "RS1")):
         ac(V("FD", k, sl(0, 128)), V(nm))
@@ -761,25 +819,22 @@ def rank_program(g, core, T, topo):
     scan(V("NS"), V("RB"), V("SEEDS"), A.mult, A.add)
     ts(V("AL"), V("NS"), 0.5, A.is_gt)
     tc(V("HHL", sl(0, 16)), V("NN"))
-    for _ in unpack(1):
-        pass
     tt(V("VMV"), V("WV", sl(16, 272)), V("AL"), A.mult)
     tt(V("VMC"), V("WC"), V("AL"), A.mult)
     for b in range(16):
         mm(V("PT", sl(b, 256, 16)), V("Rhi", sl(b * 128, b * 128 + 128)), V("HHL", sl(0, 16)), True, True)
     ac(V("ON"), V("PT", sl(0, 256)))
     dma("sp", "dout", 64, (T["yn"][:], "yn", 0, 1), (T["ON"][0:128:16, :], "ON", 0, 256))
-    fin, ft = ("FIN", "OHT"), ("FT", "FU")
+    ft = ("FT", "FU")
     for k, vm in enumerate(("VMV", "VMC")):
-        run("dve", lambda e: e.transpose(V(fin[k])[0], V(vm)[0]), [V(fin[k])], [V(vm)])
+        run("dve", lambda e: e.transpose(V(ft[k])[0], V(vm)[0]), [V(ft[k])], [V(vm)])
     for k in range(2):
-        tc(V(ft[k], sl(0, 8), sl(0, 2), sl(0, 16)), V(fin[k]))
         for eta in range(2):
-            o = V("PZ%d" % k, 0, sl(eta * 128, eta * 128 + 128))
+            o = half("PZ%d" % k, eta)
             mm(o, V("FD", eta, sl(0, 128)), V(ft[k], sl(0, 8), eta, sl(0, 16)), True, False)
             mm(o, V("FD", 2 + eta, sl(0, 128)), V(ft[k], sl(0, 8), 1 - eta, sl(0, 16)), False, True)
     for k, y in enumerate(("yv", "yc")):
         for eta in range(2):
-            tc(V("FO%d" % k, sl(0, 8), eta, sl(0, 16)), V("PZ%d" % k, 0, sl(eta * 128, eta * 128 + 128)))
+            tc(V("FO%d" % k, sl(0, 8), eta, sl(0, 16)), half("PZ%d" % k, eta))
         dma("sp", "dout", 64, (T[y][:], y, 0, 1), V("FO%d" % k, sl(0, 8), sl(0, 2), sl(0, 16)))
     finish()

import numpy as np
from concourse.mybir import dt, AluOpType as A, AxisListType, ActivationFunctionType as F

ST = 5
B2, F4, I4, U2, H2 = "bfloat16", "float32", "int32", "uint16", "float16"
SCRATCH = {}
SHAPE = {}
PLACE = {}


def _sb(name, shape, dtype, where="sbuf"):
    SCRATCH[name] = (where, shape, dtype)
    SHAPE[name] = shape


def _pack(name, width, dtype):
    box = "box_" + dtype
    at = SCRATCH[box][1][1] if box in SCRATCH else 0
    SCRATCH[box] = ("sbuf", [128, at + (width + 15) // 16 * 16], dtype)
    SHAPE[name] = [128, width]
    PLACE[name] = (box, at)


for _n, _w in (("X", 2304), ("E", 2048), ("Ec", 2048), ("E8", 2048),
               ("wE", 2048), ("Rhi", 2048), ("Rlo", 2048), ("Rr", 2048), ("ID", 128), ("NEGI", 128), ("ID2", 128), ("NEGH", 128), ("IDK", 128), ("BO", 128),
               ("RV0", 128), ("RV1", 128), ("RS0", 128), ("RS1", 128), ("D01", 128), ("S23", 128), ("ONES", 128), ("G8", 128), ("STA", 128),
               ("RB", 256), ("SEEDP", 256), ("SEEDG", 256), ("SEEDS", 256), ("SHS", 256), ("LC", 256),
               ("M2", 256), ("PRE", 256), ("OHG", 256), ("DM", 256), ("EQD", 256),
               ("NF", 256), ("MS", 256), ("G1", 256), ("G2", 256), ("G3", 256), ("PG1", 256), ("PG2", 256),
               ("CB", 256), ("BS", 256), ("BT", 256), ("N192", 256), ("LNB", 258), ("HHL", 32), ("CLB", 1), ("NG", 16), ("NH", 16)):
    (_pack if _w <= 258 else lambda n, w, d: _sb(n, [128, w], d))(_n, _w, B2)
for _n in ("M1", "NS", "SK", "GT", "Q0N", "SHF"):
    _pack(_n, 256, B2)
for _n, _w in (("CC", 16), ("KM", 256), ("RF", 256), ("POS0", 256), ("POS1", 256), ("II", 256), ("TPk0", 256), ("TPk1", 256),
               ("TPn0", 256), ("TPn1", 256), ("IC", 16), ("DD", 16), ("OHT", 256), ("OHPP", 256), ("REST", 16), ("R84", 16), ("RS", 16), ("NT", 16), ("NN", 16), ("LIVE", 16),
               ("NR", 16), ("CL", 16), ("GR", 16), ("Ta", 16), ("Tb", 16), ("Td", 16), ("Te", 16), ("QM", 16),
               ("TK", 16), ("HE", 16), ("HG", 16), ("HAS", 16), ("A0", 16), ("DAB", 16), ("lim", 1), ("thc", 1), ("cls", 1),
               ("t1", 16), ("FIN", 256), ("VMV", 256), ("VMC", 256), ("AL", 256), ("VKS", 256), ("VNS", 256), ("VKT", 256), ("VNT", 256),
               ("Tc", 16), ("HEM", 256), ("SDM", 256), ("DD1", 16), ("OFS", 256)):
    _pack(_n, _w, F4)
_sb("ON", [128, 256], F4)
for _n, _w in (("VI", 512), ("LNI", 257), ("WTI", 1)):
    _sb(_n, [128, _w], I4)
for _n, _w in (("WV", 272), ("WC", 256), ("VJ", 512), ("VL", 512), ("im", 128), ("imh", 128), ("ip", 1), ("ii", 8), ("i8", 8),
               ("KI", 16), ("OFI", 16), ("QK", 16), ("OF0", 16), ("UI", 16), ("SQ", 16), ("HI", 16), ("HP", 32), ("ci", 1)):
    _pack(_n, _w, I4)
for _n, _w in (("VU", 256), ("CU", 256), ("OFU", 16), ("OFN", 16), ("OFP", 16), ("OFH", 16), ("OFB", 16), ("V0U", 16), ("SRCU", 208), ("SRCL", 48),
               ("HR", 256), ("VR", 256), ("OFG", 8)):
    _pack(_n, _w, U2)
_sb("H16", [128, 16], H2)
_sb("V16", [128, 16], H2)
_sb("HL", [128, 4, 8, 2, 16], B2)
_sb("FT", [128, 8, 2, 16], F4)
_sb("FU", [128, 8, 2, 16], F4)
_sb("HX", [128, 2, 8, 2, 16], H2)
_sb("FO0", [128, 8, 2, 16], F4)
_sb("FO1", [128, 8, 2, 16], F4)
_sb("FD", [128, 4, 128], F4)
_sb("EQ", [128, 16, 256], B2)
_sb("EV", [128, 16, 256], B2)
_sb("WIN", [128, 8704], B2)
_sb("XV", [128, 4096], B2)
_sb("XC", [128, 4096], B2)
_sb("SRC", [128, 16, 16], F4)
_sb("SRT", [128, 16, 3], F4)
_sb("NLa", [128, 3328], B2)
_sb("NLb", [128, 768], B2)
for _n in ("Z", "Z2"):
    _sb(_n, [128, 16, 16, 16], B2)
for _t in range(ST):
    _sb("YM%d" % _t, [128, 272], B2)
    _sb("YR%d" % _t, [128, 272], B2)
    _sb("SM%d" % _t, [128, 16], F4)
    _sb("SR%d" % _t, [128, 16], F4)
    _sb("KM%d" % _t, [128, 32], F4)
    _sb("KR%d" % _t, [128, 32], F4)
    _sb("PD%d" % _t, [128, 4, 256], B2, "dram")
    _sb("PI%d" % _t, [128, 4, 256], B2, "dram")
for _t in range(4):
    _sb("PZ%d" % _t, [128, 16, 2, 16], F4, "psum")
_sb("PQ", [128, 16, 32], F4, "psum")
for _n in ("PK", "PS", "PT"):
    _sb(_n, [128, 512], F4, "psum")
SEMAPHORES = ["q_pe", "q_dve", "q_act", "q_g", "loc", "dv", "dc", "dx", "dln", "dwt", "pst", "dout", "de8"]
for _t in range(ST):
    SEMAPHORES += ["po%d" % _t, "pw%d" % _t, "pi%d" % _t, "am%d" % _t, "ay%d" % _t, "as%d" % _t, "ak%d" % _t]
SENT = (("PI", "am", 0), ("YR", "ay", 1), ("KR", "ak", 1), ("SR", "as", 1))

_RANGE = {}


def _span(name, idx):
    key = name + repr(idx)
    if key not in _RANGE:
        shape = SHAPE[name][1:]
        a = np.arange(int(np.prod(shape))).reshape(shape)[idx]
        _RANGE[key] = (sum(1 << int(k) for k in a.ravel()), None)
    return _RANGE[key]


def _bits(lo, hi):
    return lo if hi is None else (1 << min(hi, 16384)) - (1 << lo)


def _queues(g, core, T):
    eng = {"pe": g.tensor, "dve": g.vector, "act": g.scalar, "g": g, "sp": g.sync}
    cnt = {"pe": 0, "dve": 0, "act": 0, "g": 0}
    known = {q: {} for q in eng}
    vc, recs, total = {}, {}, {}

    def V(name, *idx):
        lo, hi = _span(name, idx) if idx else (0, 1 << 20)
        if name in PLACE:
            box, at = PLACE[name]
            k = idx[0] if idx else slice(0, SHAPE[name][1])
            return (T[box][:, at + k.start:at + k.stop:k.step or 1], name, lo, hi)
        return (T[name][(slice(None),) + idx] if idx else T[name][:], name, lo, hi)

    def deps(q, outs, ins, own=None):
        need = {}
        for lst, wr in ((ins, 0), (outs, 1)):
            for (_, name, lo, hi) in lst:
                psum = SCRATCH.get(name, ("",))[0] == "psum"
                m = _bits(lo, hi)
                for r in recs.get(name, ()):
                    if (q == "pe" and r[4] == "pe") or r[3][0] == own:
                        continue
                    if psum and r[4] != q:
                        hit = True
                    else:
                        hit = r[0] & m and (r[2] or wr)
                    if hit:
                        s, v = r[3]
                        if known[q].get(s, 0) < v and need.get(s, 0) < v:
                            need[s] = v
        for s in sorted(need):
            for s2, v2 in need.items():
                if s2 != s and vc.get((s2, v2), {}).get(s, 0) >= need[s]:
                    need[s] = 0
        for s in sorted(need):
            v = need[s]
            if v:
                eng[q].wait_ge(T.sem[s], v)
                known[q][s] = v
                for s2, v2 in vc.get((s, v), {}).items():
                    if known[q].get(s2, 0) < v2:
                        known[q][s2] = v2

    def note(q, tok, outs, ins):
        for (_, name, lo, hi) in ins:
            l = recs.setdefault(name, [])
            m = _bits(lo, hi)
            l[:] = [r for r in l if not (not r[2] and r[4] == q and not r[0] & ~m)]
            l.append((m, 0, 0, tok, q))
        for (_, name, lo, hi) in outs:
            l = recs.setdefault(name, [])
            psum = SCRATCH.get(name, ("",))[0] == "psum"
            m = _bits(lo, hi)
            l[:] = [r for r in l if r[0] & ~m or (psum and r[4] != q)]
            if psum:
                l[:] = [r for r in l if r[4] == q] + [r for r in l if r[4] != q and known[q].get(r[3][0], 0) < r[3][1]]
            l.append((m, 0, 1, tok, q))

    def run(q, call, outs, ins):
        deps(q, outs, ins)
        cnt[q] += 1
        s = "q_" + q
        call(eng[q]).then_inc(T.sem[s], 1)
        tok = (s, cnt[q])
        d = dict(known[q])
        d[s] = cnt[q]
        vc[tok] = d
        note(q, tok, outs, ins)

    def dma(q, sem, n, out, in_):
        deps(q, [out], [in_], sem)
        eng[q].dma_start(out[0], in_[0]).then_inc(T.sem[sem], 16)
        total[sem] = n
        vc.setdefault((sem, n), dict(known[q]))
        note("dma", (sem, n), [out], [in_])

    def arrive(name, sem, n):
        total[sem] = n
        note("ext", (sem, n), [(None, name, 0, 1 << 20)], [])

    def before(q, ins):
        deps(q, [], ins)

    def finish():
        for q in cnt:
            if cnt[q] and known["g"].get("q_" + q, 0) < cnt[q]:
                g.wait_ge(T.sem["q_" + q], cnt[q])
        for s in sorted(total):
            if known["g"].get(s, 0) < total[s]:
                g.wait_ge(T.sem[s], total[s])

    return V, run, dma, arrive, before, finish, total


def _send(core, T, topo, g, out, in_, arrived, dst):
    e = topo.engines(core, dst)[:8]
    rid, pid = topo.addr(dst, core)
    g.remote_dma(out, in_, T.sem[arrived], T.sem["loc"], pid, rid, sum(1 << k for k in e))
    return len(e)


def _relays(core, dst, topo):
    if topo.may_write(core, dst):
        return []
    c = [k for k in topo.cores_of(core) if k != core and topo.may_write(k, dst)]
    c.sort(key=lambda k: (topo.die(k) != topo.die(core), k))
    return [c[0], c[1 % len(c)]]


def _relay_program(g, core, T, topo):
    loc = 0
    for t in range(ST):
        for r, src in enumerate(T.cores):
            dst = T.cores[(r + 1 + t % 7) % len(T.cores)]
            rl = _relays(src, dst, topo)
            if core not in rl:
                continue
            n = len(topo.engines(src, core)[:8])
            for name, sem, via in SENT:
                if rl[via] == core:
                    g.wait_ge(T.sem[sem + str(t)], n)
                    loc += _send(core, T, topo, g, T[name + str(t)][:], T[name + str(t)][:], sem + str(t), dst)
    if loc:
        g.wait_ge(T.sem["loc"], loc)


def rank_program(g, core, T, topo):
    rank = T.rank_of(core)
    if rank is None:
        return _relay_program(g, core, T, topo)
    V, run, dma, arrive, before, finish, total = _queues(g, core, T)
    n_loc = [0]
    sl = slice
    ALL = sl(0, 16)
    X_ALL, X_WIN = (sl(0, 2304),), (sl(0, 2048),)

    def mm(out, lhsT, rhs, a, z):
        run("pe", lambda e: e.matmul(out[0], lhsT[0], rhs[0], a, z), [out], [lhsT, rhs])

    def ts(out, in0, s1, op0, s2=None, op1=None, more=()):
        ins = [in0] + [s for s in (s1, s2) if isinstance(s, tuple)] + list(more)
        a1 = s1[0] if isinstance(s1, tuple) else s1
        a2 = s2[0] if isinstance(s2, tuple) else s2
        if op1 is None:
            run("dve", lambda e: e.tensor_scalar(out[0], in0[0], a1, None, op0), [out], ins)
        else:
            run("dve", lambda e: e.tensor_scalar(out[0], in0[0], a1, a2, op0, op1), [out], ins)

    def tt(out, a, b, op, more=()):
        run("dve", lambda e: e.tensor_tensor(out[0], a[0], b[0], op), [out], [a, b] + list(more))

    def tc(out, in_):
        run("dve", lambda e: e.tensor_copy(out[0], in_[0]), [out], [in_])

    def ac(out, in_, f=F.Copy, scale=1.0, more=()):
        ins = [in_] + ([scale] if isinstance(scale, tuple) else []) + list(more)
        sc = scale[0] if isinstance(scale, tuple) else scale
        run("act", lambda e: e.activation(out[0], in_[0], f, scale=sc), [out], ins)

    def scan(out, d0, d1, op0, op1):
        run("dve", lambda e: e.tensor_tensor_scan(out[0], d0[0], d1[0], 0.0, op0, op1), [out], [d0, d1])

    def fill(out, c):
        run("dve", lambda e: e.memset(out[0], c), [out], [])

    def iota(out, pattern, base=0, cm=0):
        run("g", lambda e: e.iota(out[0], pattern, base, cm, allow_small_or_imprecise_dtypes=True), [out], [])

    def at(win, off):
        return (win[0].indirect(off[0]),) + win[1:]

    def gather(q, out, win, off, scale=1.0):
        if q == "act":
            ac(out, at(win, off), F.Copy, scale, [off])
        elif scale != 1.0:
            ts(out, at(win, off), scale, A.mult, more=[off])
        else:
            run("dve", lambda e: e.tensor_copy(out[0], at(win, off)[0]), [out], [win, off])

    def col(k):
        return V("CC", sl(k, k + 1))

    def top8(name, lo, hi):
        if name in PLACE:
            box, a = PLACE[name]
            return (T[box][0:8, a + lo:a + hi], name, lo, hi)
        return (T[name][0:8, lo:hi], name, lo, hi)

    def small(out, mats, rhs_name, n16):
        for b in range(16):
            mm(out, V(mats, sl(b * 128, b * 128 + 128)), V(rhs_name, sl(b, n16, 16)), b == 0, b == 15)

    def spread(h16):
        for b in range(16):
            mm(V("PT", sl(256 + b, 512, 16)), V("Rr", sl(b * 128, b * 128 + 128)), V(h16), True, True)

    AND, SHR = A.bitwise_and, A.arith_shift_right

    dma("sp", "dv", 16, V("VI", sl(0, 256)), (T["vl"][:], "vl", 0, 1))
    dma("sp", "dc", 16, V("VI", sl(256, 512)), (T["cl"][:], "cl", 0, 1))
    dma("sp", "dx", 16, V("X", sl(0, 2048)), (T["xc"][:], "xc", 0, 1))
    dma("sp", "dwt", 16, V("WTI"), (T["wt"][:], "wt", 0, 1))
    fill(V("LNI"), 0)
    for out_sl, nm in ((sl(0, 256), "ln"), (sl(256, 257), "th")):
        o = V("LNI", out_sl)
        dma("sp", "dln", 32, (T["LNI"][0:128:16, out_sl], "LNI", o[2], o[3]), (T[nm][:], nm, 0, 1))
    iota(V("im"), [[1, 128]])
    iota(V("ip"), [[0, 1]], 0, 1)
    iota(V("LC"), [[16, 256]])
    iota(V("IC"), [[16, 16]])
    iota(V("RF"), [[0, 16], [1, 16]])
    iota(V("II"), [[16, 16], [0, 16]])
    iota(V("POS0"), [[16, 16], [-256, 16]], 3840)
    iota(V("POS1"), [[256, 16], [16, 16]])
    iota(V("WIN", sl(0, 4352)), [[0, 4352]])
    iota(V("Rlo"), [[0, 2048]])

    i_ = lambda k: V("ii", sl(k, k + 1))
    ts(i_(0), V("ip"), 15, AND)
    ts(i_(1), V("ip"), 4, SHR)
    ts(i_(2), V("ip"), 31, AND)
    ts(i_(3), V("ip"), 4, SHR, 1, AND)
    tc(col(0), V("ip"))
    ts(V("imh"), V("im"), 4, SHR)
    tc(V("CC", sl(1, 3)), V("ii", sl(0, 2)))
    tc(col(4), i_(3))
    ts(col(3), i_(3), -1.0, A.mult, 1.0, A.add)
    ts(col(5), i_(0), -2.0, A.mult, 15.0, A.add)
    ts(col(6), i_(2), -2.0, A.mult, 31.0, A.add)
    ts(V("ID"), V("im"), col(0), A.is_equal)
    ts(V("CC", sl(5, 7)), V("CC", sl(5, 7)), col(0), A.add)
    ts(V("BO"), V("imh"), col(2), A.is_equal)
    ts(col(7), i_(0), 1.5, A.is_le)
    ts(col(8), i_(0), 3.5, A.is_le)
    for nm, c, h in (("RV0", 5, 3), ("RV1", 5, 4), ("RS0", 6, 3), ("RS1", 6, 4)):
        ts(V(nm), V("im"), col(c), A.is_equal, col(h), A.mult)
    tt(col(8), col(8), col(7), A.subtract)
    ts(V("NEGI"), V("im"), col(0), A.is_equal, -1.0, A.mult)
    ac(V("E"), V("X", sl(0, 2048)), F.Copy, 0.0)
    for k in range(8):
        ac(V("E", sl(16 * k, 2048, 129)), V("BO", sl(16 * k, 16 * k + 16)))
    dma("sp", "de8", 16, top8("E8", 0, 2048), (T["E"][0:128:16, :], "E", 0, 2048))
    for k in range(2):
        tc(V("HX", k, sl(0, 8), sl(0, 2), sl(0, 16)), V("VI", sl(256 * k, 256 * k + 256)))

    def payload_in():
        for k in range(2):
            h = sl(256 * k, 256 * k + 256)
            ts(V("VJ", h), V("VI", h), 1792, AND)
            ts(V("VL", h), V("VI", h), 255, AND)
            tc(V("HL", 2 * k, sl(0, 8), sl(0, 2), sl(0, 16)), V("VJ", h))
            tc(V("HL", 2 * k + 1, sl(0, 8), sl(0, 2), sl(0, 16)), V("VL", h))
        for a in range(4):
            dma("sp", "pst", 64, (T["PD0"][32 * a:32 * a + 32, :], "PD0", 1024 * a, 1024 * a + 1024), V("HL", a, sl(0, 8), sl(0, 2), sl(0, 16)))

    def to_window(name, sem, lo):
        for a in range(4):
            dma("sp", sem, 64, (T["WIN"][a:128:16, lo:lo + 4096], "WIN", lo, lo + 4096), (T[name][32 * a:32 * a + 32, :], name, 1024 * a, 1024 * a + 1024))

    def half(pz, k):
        return V(pz, sl(4 * k, 4 * k + 4))

    for k, dst in enumerate(("VU", "CU")):
        pz = "PZ%d" % k
        for kap in range(2):
            for sw in range(2):
                mm(half(pz, kap), V(("RV%d", "RS%d")[sw] % kap), V("HX", k, sl(0, 8), (kap, 1 - kap)[sw], sl(0, 16)), sw == 0, sw == 1)
        for kap in range(2):
            tc(V("FT", sl(0, 8), kap, sl(0, 16)), half(pz, kap))
        run("dve", lambda e: e.transpose(V("VMV")[0], V("FT")[0]), [V("VMV")], [V("FT")])
        tc(V(dst), V("VMV"))
        if k == 0:
            tc(V("WV", sl(16, 272)), V("VMV"))
    fill(V("WV", sl(0, 16)), 0)
    fill(V("Z", ALL, sl(0, 2)), 0.0)

    def consts_early():
        tc(col(9), V("WTI"))
        fill(V("RB"), 1.0)
        fill(V("RB", sl(0, 256, 16)), 0.0)
        fill(V("SEEDS"), 1.0)
        fill(V("LC", sl(0, 256, 16)), 16777216.0)
        fill(V("Q0N"), 0.0)
        fill(V("Q0N", sl(0, 256, 16)), -8192.0)
        lengths_in()
        for _ in start_step(0):
            pass

    def consts_mid():
        ts(V("PS", sl(256, 512)), V("RF"), col(1), A.is_gt)
        ts(V("DM"), V("RF"), col(1), A.is_lt)
        ts(V("SDM"), V("RF"), col(1), A.is_lt, -1.0, A.add)
        tc(V("RF"), V("RB"))
        fill(V("DM", sl(0, 256, 16)), 0.0)
        ts(V("ID2"), V("im"), col(0), A.is_equal, 2.0, A.mult)
        ts(V("NEGH"), V("im"), col(0), A.is_equal, -0.5, A.mult)
        ts(col(12), col(1), -16.0, A.add)
        fill(V("SEEDP"), -1.0)
        fill(V("SEEDP", sl(1, 256, 16)), 63.0)
        for nm in ("POS0", "POS1", "II", "IC"):
            ts(V(nm), V(nm), col(1), A.add)
        ts(V("D01"), V("im"), col(0), A.is_equal, col(7), A.mult)
        ts(col(10), col(0), 2.0, A.add)
        ts(V("S23"), V("im"), col(10), A.is_equal, col(7), A.mult)
        ts(col(11), col(7), 2048.0, A.mult, col(8), A.add)

    def places(m, grow):
        tt(V("OHT"), V("II"), V("POS%d" % m), A.subtract)
        ts(V("TPk%d" % m), V("OHT"), 8192.0, A.add)
        ts(V("TPn%d" % m), V("OHT"), 8448.0 - grow, A.add)

    def consts_late():
        ts(V("DD"), V("IC"), 2048.0, A.add)
        ts(V("t1"), V("im", sl(0, 16)), col(1), A.is_equal)
        for b in range(16):
            ts(V("Rr", sl(128 * b, 128 * b + 128)), V("BO"), V("t1", sl(b, b + 1)), A.mult)
        places(0, -256.0)
        fill(V("SEEDG"), -1.0)
        fill(V("SEEDG", sl(1, 256, 16)), -65.0)
        ts(V("G8"), V("G8"), col(2), A.is_equal, 4096.0, A.mult)
        ts(i_(4), V("ip"), 3, SHR, 1, AND)
        tc(col(13), i_(4))
        ts(V("OFG"), V("i8"), col(13), A.add)

    def consts_last():
        places(1, 16.0)
        ts(V("IDK"), V("im"), col(0), A.is_equal, 4096.0, A.mult)
        ts(V("DD1"), V("DD"), 1.0, A.add)
        ts(col(14), col(1), 0.5, A.is_gt)
        ts(col(15), col(14), -1.0, A.add)

    def lengths_in():
        tc(V("LNB", sl(0, 256)), V("LNI", sl(0, 256)))
        ts(V("ci"), V("LNI", sl(256, 257)), 1016, AND)
        tc(V("LNB", sl(256, 257)), V("ci"))
        ts(V("ci"), V("LNI", sl(256, 257)), 7, AND)
        tc(V("LNB", sl(257, 258)), V("ci"))
        small(V("PS", sl(80, 96)), "E", "LNB", 256)
        mm(V("PS", sl(96, 97)), V("BO"), V("LNB", sl(256, 257)), True, False)
        mm(V("PS", sl(96, 97)), V("BO"), V("LNB", sl(257, 258)), False, True)
        tc(V("NN"), V("PS", sl(80, 96)))
        tc(V("thc"), V("PS", sl(96, 97)))
        tc(V("lim"), V("thc"))

    def start_step(t):
        yield ts(V("LIVE"), V("NN"), 3.5, A.is_ge)
        yield tt(V("Tb"), V("NN"), V("LIVE"), A.mult)
        yield ts(V("SEEDS", sl(0, 256, 16)), V("Tb"), -15.0, A.add)
        yield scan(V("NS"), V("RB"), V("SEEDS"), A.mult, A.add)
        yield ts(V("M1"), V("NS"), 3.0, A.is_lt, -16777216.0, A.mult)
        yield ts(V("M2"), V("NS"), 0.5, A.is_le, 8192.0, A.mult)
        yield tc(V("YM%d" % t, sl(256, 272)), V("LIVE"))
        yield ts(V("R84"), V("LIVE"), -20.0, A.mult, -44.0, A.add)
        yield ts(V("REST"), V("LIVE"), -1.0, A.mult, 1.0, A.add)
        yield ts(V("NR"), V("LIVE"), 99.0, A.mult)
        yield ts(V("HAS"), V("NN"), 0.5, A.is_ge)
        yield ts(V("A0"), V("WV", sl(31, 272, 16)), 1.0, A.add)
        yield tt(V("NR"), V("NR"), V("NN"), A.add)

    def push(t, name, k):
        land, sem, via = SENT[k]
        dst = T.cores[(rank + 1 + t % 7) % len(T.cores)]
        rl = _relays(core, dst, topo)
        before("g", [V(name + str(t))])
        n_loc[0] += _send(core, T, topo, g, T[land + str(t)][:], T[name + str(t)][:], sem + str(t), rl[via] if rl else dst)
        total["loc"] = n_loc[0]

    def came(t, k):
        land, sem, via = SENT[k]
        src = T.cores[(rank - 1 - t % 7) % len(T.cores)]
        rl = _relays(src, core, topo)
        arrive(land + str(t), sem + str(t), len(topo.engines(rl[via] if rl else src, core)[:8]))

    def lists_in(j):
        for b in range(16):
            if j < 2:
                o, r = V("PZ3", sl(4 * j, 4 * j + 4), sl(0, 2), sl(0, 13)), V("NLa", sl(1664 * j + b, 1664 * j + 1664, 16))
            else:
                o, r = V("PZ3", sl(0, 8), sl(0, 2), sl(13, 16)), V("NLb", sl(b, 768, 16))
            mm(o, V("Ec", sl(b * 128, b * 128 + 128)), r, b == 0, b == 15)

    def unpack(k):
        h = sl(128 * k, 128 * k + 128)
        w = half("PZ3", k)
        hv = V("WV", sl(h.start + 16, h.stop + 16))
        yield ts(hv, w, 2.0 ** -11, A.mult, -0.49976, A.add)
        yield tc(V("WC", h), w)
        yield tc(V("VU", h), hv)
        yield ts(V("WC", h), V("WC", h), 2047, AND)
        yield tc(V("CU", h), V("WC", h))

    def both(a, b):
        for _ in a:
            next(b, None)
        for _ in b:
            pass

    for t in range(ST):
        md = min(t, 1)
        unit = (256.0, -16.0)[md]
        S = str(t)
        ym, sm, km = "YM" + S, "SM" + S, "KM" + S

        def gv(q, u):
            gather(q, V("XV", sl(512 * u, 512 * u + 512)), V("X", *X_WIN), V("VU", sl(32 * u, 32 * u + 32)), 0.5)

        def gc(u):
            for c in (2 * u, 2 * u + 1):
                q0 = 2 * md
                off = V("CU", sl(16 * c + q0, 16 * c + 16))
                h = sl(256 * c + 16 * q0, 256 * c + 256)
                tt(V("XC", h), at(V("X", *X_WIN), off), V("XV", h), A.subtract, [off])

        def bend(u):
            pz = "PZ%d" % (u % 4)
            for k in range(2):
                o = V(pz, sl(7 * k, 7 * k + 7))
                a = 256 * (2 * u + k)
                mm(o, V("ID"), V("XV", sl(a + 16, a + 240)), True, False)
                mm(o, V("NEGI"), V("XC", sl(a + 32, a + 256)), False, True)

        def babs(u):
            ac(V("Z", sl(2 * u, 2 * u + 2), sl(2, 16)), V("PZ%d" % (u % 4), sl(0, 14)), F.Abs, 8192.0)

        def key(c0, c1):
            if c1 == 16:
                for h in (sl(0, 16 * c0), sl(16 * c0, 256)):
                    mm(V("PK", h), V("ID"), V("M1", h), False, False)
                    mm(V("PK", h), V("ID"), V("LC", h), False, False)
            for b in range(16):
                mm(V("PK", sl(16 * c0, 16 * c1)), V("E", sl(b * 128, b * 128 + 128)), V("Z", sl(c0, c1), ALL, b), b == 0 and c0 == 0, b == 15 and c1 == 16)

        banks = ((0, 16, 12, 2), (0, 8, 8, 4), (8, 8, 8, 4), (0, 8, 4, 4), (8, 8, 4, 4), (0, 8, 0, 4), (8, 8, 0, 4))

        def dist_x(v):
            c0, nc, q0, nq = banks[v]
            for c in range(nc):
                a = 256 * (c0 + c) + 16 * q0
                mm(V("PZ%d" % (v % 4), sl(c * nq // 2, (c + 1) * nq // 2)), V("ID"), V("XV", sl(a, a + 16 * nq)), c == 0, False)

        def dist_y(v):
            c0, nc, q0, nq = banks[v]
            pz = "PZ%d" % (v % 4)
            for k in range(nq):
                mm(V(pz, sl(k // 2, 16, nq // 2), k % 2), V("NEGH"), V(ym, sl(16 * c0, 16 * (c0 + nc))), False, k == nq - 1)
            ac(V("Z2", sl(c0, c0 + nc), sl(q0, q0 + nq)), V(pz), F.Abs, 2.0)

        def dist_sum(q0, q1):
            if q1 == 14:
                mm(V("PQ", ALL, ALL), V("ID"), V("PRE"), False, False)
            for b in range(16):
                mm(V("PQ", ALL, sl(q0, q1)), V("E", sl(b * 128, b * 128 + 128)), V("Z2", ALL, sl(q0, q1), b), False, b == 15 and q0 == 0)

        if t:
            for nl, lo, hi in (("NLa", 0, 208), ("NLb", 208, 256)):
                for a in range(4):
                    dma("sp", "po" + S, 128, (T["PD" + S][32 * a:32 * a + 32, :, lo:hi], "PD" + S, 1024 * a, 1024 * a + 1024), (T[nl][a:128:16, :], nl, 0, 4096))
            push(t, "PD", 0)
            to_window("PD" + S, "pw" + S, 0)
        else:
            iota(V("SHS"), [[0, 256]])
            iota(V("G8"), [[0, 16], [1, 8]])
            iota(V("i8"), [[2, 8]])
            iota(V("ONES"), [[0, 128]], 1)
            iota(V("N192"), [[0, 256]], -192)
        gv("dve", 0)
        gv("act", 1)
        gc(0)
        bend(0)
        gv("act", 2)
        if t:
            for _ in unpack(1):
                pass
        gv("act", 3)
        gc(1)
        bend(1)
        babs(0)
        if t == 0:
            payload_in()
            push(t, "PD", 0)
            to_window("PD0", "pw0", 0)
        gv("act", 4)
        babs(1)
        gc(2)
        bend(2)
        gv("act", 5)
        gc(3)
        bend(3)
        babs(2)
        gv("act", 6)
        gc(4)
        bend(4)
        babs(3)
        gc(5)
        bend(5)
        key(0, 8)
        gv("act", 7)
        babs(4)
        gc(6)
        bend(6)
        babs(5)
        gc(7)
        key(8, 12)
        bend(7)
        babs(6)
        babs(7)
        if t == 0:
            consts_early()
            ac(V("wE"), V("E"), F.Copy, col(9))
            consts_mid()
        else:
            for _ in start_step(t):
                pass
        dist_x(0)
        dist_x(1)
        key(12, 16)
        mm(V("PQ", ALL, ALL), V("ID"), V("M2"), True, False)
        mm(V("PQ", ALL, ALL), V("ID"), V("Q0N"), False, False)
        dist_x(2)
        dist_x(3)
        scan(V("KM"), V("RF"), V("PK", sl(0, 256)), A.mult, A.max)
        tc(V("KI"), V("KM", sl(15, 256, 16)))
        ts(V("OFI"), V("KI"), 4095, AND)
        ts(V("OFU"), V("OFI"), col(1), A.add)
        ts(V("OFN"), V("OFI"), col(12), A.add)
        gather("act", V("G3"), V("XC"), V("OFU"))
        gather("dve", V("G1"), V("XV"), V("OFU"))
        gather("dve", V("G2"), V("XV"), V("OFN"))
        for k, (gm, mat) in enumerate((("G1", "ID"), ("G3", "NEGI"), ("G2", "ID2"))):
            mm(V("PT", sl(0, 256)), V(mat), V(gm), k == 0, k == 2)
        ts(V("QK"), V("OFI"), 4, SHR, 15, AND)
        ts(V(ym, sl(0, 256)), V("PT", sl(0, 256)), 0.0, A.max, 63.0, A.min)
        dist_y(0)
        small(V("PS", sl(16, 32)), "wE", ym, 256)
        for v in range(1, 4):
            dist_y(v)
        push(t, "YM", 1)
        if t == 0:
            iota(V("WIN", sl(4352, 8192)), [[0, 3840]])
        tt(V("SEEDP", sl(0, 256, 16)), V("QK"), V("R84"), A.add)
        scan(V("SK"), V("RB"), V("SEEDP"), A.mult, A.add)
        p0 = V("PK", sl(0, 256))
        ts(V(km, sl(0, 16)), V("QK"), -unit, A.mult, 4096.0 + 16.0 * unit, A.add)
        ts(p0, V("SK"), 0.0, A.is_equal)
        ts(V("PRE"), V("SK"), 1.5, A.is_le, 8192.0, A.mult)
        tt(V("VKS"), p0, V("WV", sl(16, 272)), A.mult)
        tc(V("UI"), V("PS", sl(16, 32)))
        scan(V("VKT"), V("RF"), V("VKS"), A.mult, A.add)
        ts(V("UI"), V("UI"), 2047, AND)
        tt(V("VNS"), p0, V("WV", sl(15, 271)), A.mult)
        tt(V("SQ"), V("UI"), V("UI"), A.mult)
        ts(V("Td"), V("VKT", sl(15, 256, 16)), 37.0, A.mult)
        ts(V("SQ"), V("SQ"), 5, SHR)
        scan(V("VNT"), V("RF"), V("VNS"), A.mult, A.add)
        tt(V("HI"), V("SQ"), V("Td"), A.add)
        ts(V("QM"), V("QK"), -16.0, A.add)
        ts(V("HI"), V("HI"), 2047, AND)
        ts(V(km, sl(16, 32)), V("VNT", sl(15, 256, 16)), 1.0, A.add)
        tc(V("H16"), V("HI"))
        push(t, "KM", 2)
        if t == 0:
            ts(V("OF0"), V("QK"), -256.0, A.mult, 3840.0, A.add)
            tt(V("Ta"), V("OF0"), V("IC"), A.add)
            tc(V("OFP"), V("Ta"))
            consts_late()
        off = ("OFP", "OFU")[md]
        for v in range(4, 7):
            dist_x(v)
            dist_y(v)
            if v == 5:
                spread("H16")
        dist_sum(8, 14)
        dist_sum(4, 8)
        if t == 0:
            ac(V("Rhi"), V("X", sl(0, 2048)), F.Copy, 0.0)
            for k in range(8):
                ac(V("Rhi", sl(16 * k, 2048, 128)), V("ID", sl(16 * k, 16 * k + 16)))
                ac(V("Rlo", sl(16 * k + 1, 2048, 128)), V("ID", sl(16 * k, 16 * k + 16)))
        gather("act", V("PG1"), V("WIN", sl(0, 4096)), V(off))
        gather("act", V("PG2"), V("WIN", (sl(256, 4352), sl(0, 4096))[md]), V(("OFP", "OFN")[md]))
        dist_sum(0, 4)
        tc(V("HG"), V("HI"))
        tt(V("OHT"), p0, V("TPk%d" % md), A.mult)
        ts(V("HP", sl(0, 16)), V("HI"), 1792, AND)
        ts(V("HP", sl(16, 32)), V("HI"), 255, AND)
        ts(V("GT"), V("SK"), 0.5, A.is_gt)
        tc(V("HHL"), V("HP"))
        tt(V("OHPP"), V("OHT"), V("POS%d" % md), A.add)
        tc(V("HR"), V("PT", sl(256, 512)))
        for c in range(16):
            ts(V("EQ", c, sl(0, 256 - 16 * c)), V("HR", sl(16 * c, 256)), V("HG", sl(c, c + 1)), A.is_equal)
        d = V("EQ", ALL, ALL)
        tt(d, d, V("PS", sl(256, 512)), A.mult)
        ex = V("PK", sl(0, 256))
        mm(ex, V("D01"), V("PG1"), True, False)
        mm(ex, V("S23"), V("PG2"), False, True)
        mm(V("PK", sl(256, 512)), V("S23"), V("PG1"), True, False)
        for b in range(16):
            for k, mat in enumerate(("Rhi", "Rlo")):
                mm(V("PK", sl(256 + b, 512, 16)), V(mat, sl(b * 128, b * 128 + 128)), V("HHL", sl(16 * k, 16 * k + 16)), False, b == 15 and k == 1)
        ac(V("WIN", sl(8192, 8704)), V("PK"))
        if t == 0:
            ac(V("Ec"), V("E"), F.Copy, col(11))
        ts(V("NF"), V("PQ", ALL, ALL), V("lim"), A.is_gt)
        scan(V("MS"), V("NF"), V("NF"), A.mult, A.add)
        M = V("MS", sl(15, 256, 16))
        ts(V("CL"), M, 15.5, A.is_le)
        tt(V("Ta"), M, V("QM"), A.add)
        tt(V("GR"), V("LIVE"), V("CL"), A.subtract)
        SZ = V(sm)
        tt(SZ, V("Ta"), V("CL"), A.mult)
        push(t, "SM", 3)
        tt(V("STA"), at(V("GR"), V("OFG")), V("G8"), A.mult, [V("OFG")])
        ts(V("NG"), V("GR"), -4096.0, A.mult, 4096.0, A.add)
        for c in range(16):
            mm(top8("PT", 16 * c, 256), V("STA", sl(8 * c, 8 * c + 8)), V("EQ", c, sl(0, 256 - 16 * c)), c == 0, c == 15)
        oh = V("PS", sl(32, 48))
        mm(oh, V("ID"), V("H16"), True, False)
        mm(oh, V("ID"), V("NG"), False, False)
        ph = V("PQ", ALL, sl(16, 32))
        for k in range(3):
            came(t, k)
        to_window("PI" + S, "pi" + S, 4096)
        ts(V("Tb"), V("GR"), -256.0, A.mult, 320.0, A.add)
        tt(V("Ta"), SZ, V("GR"), A.subtract)
        tt(V("SEEDG", sl(0, 256, 16)), V("Tb"), V("QK"), A.add)
        ts(V("Ta"), V("Ta"), unit, A.mult)
        tt(V("RS"), V("KR" + S, ALL), V("REST"), A.mult)
        scan(V("OHG"), V("RB"), V("SEEDG"), A.mult, A.add)
        tt(V("SHS", sl(0, 256, 16)), V("Ta"), V("RS"), A.add)
        ts(ph, V("OHG"), 1.0, A.is_equal)
        run("dve", lambda e: e.tensor_reduce(V("cls")[0], V("CL")[0], AxisListType.X, A.add), [V("cls")], [V("CL")])
        tt(ph, ph, V("TPn%d" % md), A.mult)
        tc(V("CLB"), V("cls"))
        tt(ph, ph, V("OHPP"), A.add)
        cb = top8("CB", 0, 256)
        tc(cb, top8("PT", 0, 256))
        for b in range(16):
            box, a = PLACE["CB"]
            mm(oh, top8("E8", 128 * b, 128 * b + 128), (T[box][0:8, a + b:a + 256:16],) + cb[1:], False, b == 15)
        scan(V("SHF"), V("GT"), V("SHS"), A.mult, A.add)
        tt(V("HAS"), V("HAS"), V("YR" + S, sl(256, 272)), A.mult)
        tt(V("SRC"), ph, V("SHF"), A.add)
        tt(V("A0"), V("A0"), V("HAS"), A.mult)
        ts(V("SRCU"), V("SRC", ALL, sl(0, 13)), 8703.0, A.min)
        tt(V("DAB"), V("KR" + S, sl(16, 32)), V("A0"), A.subtract)

        def early(c0, c1):
            gather("act", V("NLa", sl(208 * c0, 208 * c1)), V("WIN"), V("SRCU", sl(13 * c0, 13 * c1)))

        early(0, 8)
        early(8, 12)
        tt(V("t1"), oh, V("DD"), A.min)
        tt(V("NN"), V("NN"), V("GR"), A.add)
        tc(V("OFH"), V("t1"))
        ts(V("NN"), V("NN"), 16.0, A.min)
        mm(V("PS", sl(64, 65)), V("ONES"), V("CLB"), True, True)
        xw = V("X", *X_ALL)
        run("dve", lambda e: e.tensor_copy(at(xw, V("OFH"))[0], T[ym][:, 0:256]), [xw], [V("OFH"), V(ym, sl(0, 256))])
        tt(V("NN"), V("NN"), SZ, A.subtract)
        tc(V("ci"), V("PS", sl(64, 65)))
        if t == 0:
            consts_last()
        ts(V("ci"), V("ci"), 31, AND)
        came(t, 3)
        sr = V("SR" + S)
        tt(V("TK"), sr, V("NR"), A.is_gt)
        tt(V("NT"), sr, V("NR"), A.is_le)
        tt(V("Tc"), V("DAB"), V("TK"), A.mult)
        tt(V("NT"), V("NT"), V("RS"), A.mult)
        tt(V("V16"), V("Tc"), V("A0"), A.add)
        spread("V16")
        lists_in(0)
        for k in range(3):
            tt(V("SRT", ALL, k), V("SRC", ALL, 13 + k), V("NT"), A.subtract)
        tt(V("HE"), V("Tc"), V("A0"), A.add)
        ts(V("SRCL"), V("SRT"), 8703.0, A.min)
        gather("act", V("NLb"), V("WIN"), V("SRCL"))
        early(12, 16)
        ts(V("SDM", sl(0, 256, 16)), V("HE"), col(14), A.mult, col(15), A.add)
        ts(V("V0U"), V("HE"), -1.0, A.add)
        scan(V("HEM"), V("DM"), V("SDM"), A.mult, A.add)
        ts(V("NH"), V("HE"), 0.5, A.is_lt)
        tc(V("VR"), V("PT", sl(256, 512)))
        tt(V("EQD"), V("PT", sl(256, 512)), V("HEM"), A.is_equal)
        mm(V("PK", sl(0, 256)), V("IDK"), V("EQD"), True, False)
        mm(V("PK", sl(0, 256, 16)), V("ID"), V("V16"), False, False)
        mm(V("PK", sl(0, 256, 16)), V("IDK"), V("NH"), False, False)
        for c in range(15, 0, -1):
            ts(V("EV", c, sl(0, 16 * c)), V("VR", sl(0, 16 * c)), V("HE", sl(c, c + 1)), A.is_equal)
            mm(V("PK", sl(16 * c, 256)), V("IDK"), V("EV", sl(c, 16), sl(16 * c - 16, 16 * c)), False, c == 1)
        tt(V("BS"), at(V("X", *X_WIN), V("V0U")), V("YR" + S, sl(0, 256)), A.add, [V("V0U")])
        lists_in(2)
        scan(V("OFS"), V("RF"), V("PK", sl(0, 256)), A.mult, A.add)
        ts(V("BT"), V("BS"), 0.5, A.mult, 191.75, A.add)
        tt(V("t1"), V("OFS", sl(15, 256, 16)), V("DD1"), A.min)
        tt(V("Ta"), sr, V("NN"), A.subtract)
        ts(V("OFB"), V("t1"), -1.0, A.add)
        tt(at(xw, V("OFB")), V("BT"), V("N192"), A.add, [V("OFB")])

        def lengths():
            yield tt(V("lim"), V("ci"), V("thc"), A.add)
            yield tt(V("Ta"), V("Ta"), V("TK"), A.mult)
            yield tt(V("NN"), V("NN"), V("Ta"), A.add)

        both(unpack(0), lengths())
        lists_in(1)
    for _ in unpack(1):
        pass
    dma("sp", "dout", 64, (T["yx"][:], "yx", 0, 1), V("X", sl(0, 2048)))
    for k, nm in enumerate(("RV0", "RV1", "RS0", "RS1")):
        ac(V("FD", k, sl(0, 128)), V(nm))
    ts(V("SEEDS", sl(0, 256, 16)), V("NN"), -15.0, A.add)
    scan(V("NS"), V("RB"), V("SEEDS"), A.mult, A.add)
    ts(V("AL"), V("NS"), 0.5, A.is_gt)
    tc(V("HHL", sl(0, 16)), V("NN"))
    tt(V("VMV"), V("WV", sl(16, 272)), V("AL"), A.mult)
    tt(V("VMC"), V("WC"), V("AL"), A.mult)
    for b in range(16):
        mm(V("PT", sl(b, 256, 16)), V("Rhi", sl(b * 128, b * 128 + 128)), V("HHL", sl(0, 16)), True, True)
    ac(V("ON"), V("PT", sl(0, 256)))
    dma("sp", "dout", 64, (T["yn"][:], "yn", 0, 1), (T["ON"][0:128:16, :], "ON", 0, 256))
    ft = ("FT", "FU")
    for k, vm in enumerate(("VMV", "VMC")):
        run("dve", lambda e: e.transpose(V(ft[k])[0], V(vm)[0]), [V(ft[k])], [V(vm)])
    for k in range(2):
        for eta in range(2):
            o = half("PZ%d" % k, eta)
            mm(o, V("FD", eta, sl(0, 128)), V(ft[k], sl(0, 8), eta, sl(0, 16)), True, False)
            mm(o, V("FD", 2 + eta, sl(0, 128)), V(ft[k], sl(0, 8), 1 - eta, sl(0, 16)), False, True)
    for k, y in enumerate(("yv", "yc")):
        for eta in range(2):
            tc(V("FO%d" % k, sl(0, 8), eta, sl(0, 16)), half("PZ%d" % k, eta))
        dma("sp", "dout", 64, (T[y][:], y, 0, 1), V("FO%d" % k, sl(0, 8), sl(0, 2), sl(0, 16)))
    finish()
